import numpy as np, ml_dtypes
CORES = [48,51,52,55]
N = 4
BF = ml_dtypes.bfloat16
W, B, RO, NEED = 4096, 256, 4, 9
def spot(o, u, t):
    return (((o * (2 * u + 1)) >> 5) + o + 77 * t) & (W - 1)
def base(rng):
    amp = rng.integers(32, 256, (N, 8, 1, W))
    return {"hue": (rng.random((N, 8, 16, W)) * (amp + 1)).astype(np.int64), "own": rng.integers(0, W, (N, 8, 16, B)), "nb": rng.integers(0, B, (N, 8, 16, B)),
            "tau": rng.integers(0, B, (N, 8, B)), "prev": rng.integers(0, B, (N, 8, B)), "foe": rng.integers(0, B, (N, 8, B)),
            "tas": rng.integers(0, 1024, (N, 8, B)), "wt": rng.integers(0, 256, (N, 8, 16, 1))}
def pack(d):
    out = {"hue": np.ascontiguousarray(d["hue"].reshape(N, 128, W)).astype(np.float32).astype(BF)}
    for k in ("own", "nb"): out[k] = np.ascontiguousarray(d[k].reshape(N, 128, B)).astype(np.int32)
    for k in ("tau", "prev", "foe", "tas"): out[k] = np.ascontiguousarray(d[k]).astype(np.int32)
    out["wt"] = np.ascontiguousarray(d["wt"].reshape(N, 128, 1)).astype(np.int32)
    return out
def setup_inputs(rng):
    return pack(base(rng))
def setup_inputs_ties(rng):
    d = base(rng)
    e = rng.choice(np.array([3.0, 6.0, 12.0]), (N, 8, 1, W)); m = rng.choice(np.array([1, 17, 85]), (N, 8, 1, 1)); m[0, 0] = 85; m[0, 1] = 1
    d["hue"] = np.minimum((4 * rng.random((N, 8, 16, W)) ** e).astype(np.int64), 3) * m
    pool = rng.integers(0, W, (N, 8, 24)); some = np.take_along_axis(pool, rng.integers(0, 24, (N, 8, 16 * B)), 2).reshape(N, 8, 16, B)
    d["own"][:, 1::2] = some[:, 1::2]; d["tas"][:, 1::2] = rng.choice(np.array([5, 512, 1000]), (N, 4, B))
    for a in (2, 5):
        d["own"][:, a, :, 1::2] = d["own"][:, a, :, 0::2]; d["tas"][:, a, 1::2] = d["tas"][:, a, 0::2]
    pool = rng.integers(0, B, (N, 8, 20)); few = np.take_along_axis(pool, rng.integers(0, 20, (N, 8, B)), 2)
    d["tau"][:, 3:] = few[:, 3:]
    return pack(d)
def setup_inputs_corners(rng):
    d = base(rng); b = np.arange(B)
    pats = np.stack([0 * b, 0 * b + B - 1, b, B - 1 - b, (b + 1) % B, (B - 1) * (b & 1), b >> 1, np.minimum(b + 1, B - 1)])
    ia = np.arange(8)[None, :] + np.arange(N)[:, None] + rng.integers(0, 8)
    d["tau"] = pats[ia & 7]; d["prev"] = pats[(ia + 3) & 7]; d["foe"] = pats[(ia + 5) & 7]; d["nb"] = pats[(ia[:, :, None] + np.arange(16)) & 7]
    d["tau"][0] = np.argsort(rng.random((8, B)), axis=1)
    d["tau"][0, :4] = np.stack([b, B - 1 - b, (b + 1) % B, (b + B - 1) % B])
    d["tau"][0, 6, 0] = d["tau"][0, 6, 1]
    d["hue"][0] = 128 + (d["hue"][0] >> 1); d["hue"][1] = d["hue"][1] & 1
    d["hue"][2] = 255; d["hue"][3, 7] = 255; d["tau"][2] = np.argsort(rng.random((8, B)), axis=1)
    kind = rng.integers(0, 5, (N, 8, 1, B)); one = d["own"][:, :, :1, :]; two = (W - 1) * rng.integers(0, 2, (N, 8, 16, B))
    o = d["own"]; o = np.where(kind == 0, 0, np.where(kind == 1, W - 1, np.where(kind == 2, one, np.where(kind == 3, two, o)))); d["own"] = o
    d["tas"] = np.where(rng.random((N, 8, B)) < 0.5, rng.choice(np.array([0, 1, 511, 512, 1023]), (N, 8, B)), d["tas"])
    d["wt"][:, 0] = 0; d["wt"][:, 7] = 255
    return pack(d)
def setup_inputs_close(rng):
    d = base(rng); b = np.arange(B); p = rng.permutation(N); s, m = int(p[0]), int(p[1]); o, u = d["own"], d["tas"]
    hn = (NEED - 1) // 2; nn = max(NEED, 17 - NEED); ca = int(spot(W - 1, 0, 0)); last = int(spot(W - 1, 1023, RO - 1))
    x = np.minimum(d["hue"], 253)
    x[:, 2:4, :, ca] = 254
    for a, lo in ((2, B - 1), (3, B // 2)):
        c = spot(o[:, a], u[:, a, None, :], 0); o[:, a] = np.where(c == ca, 0, o[:, a])
        o[:, a, 3, lo:] = W - 1; u[:, a, lo:] = 0
        d["tau"][:, a] = rng.integers(lo, B, (N, 1))
    x[:, 4, NEED - 1:] = 7; d["tau"][:, 4] = b; d["prev"][:, 4] = B - 1 - b
    for a, lo in ((5, 129), (6, 250)):
        x[:, a] = 0
        x[:, a, :hn] = lo + rng.integers(0, 4, (N, hn, W)); x[:, a, 8:8 + hn] = lo + rng.integers(0, 4, (N, hn, W))
        x[m, a] = rng.integers(0, 2, (16, W))
    x[:, 7, nn:, last] = 255; x[:, 7, nn:, W - 1] = 0
    o[:, 7] = np.where(np.argsort(rng.random((N, 16, B)), axis=1) < 10, W - 1, o[:, 7])
    x[s] = rng.integers(0, 16, (8, 16, W)); x[s, :, :nn] = 255
    u[s, 7] = 1023; d["wt"][s, 7] = 0; d["wt"][s, 7, 0, 0] = 255; d["wt"][s, 7, 1, 0] = 2
    d["hue"] = x
    return pack(d)
def setup_inputs_spread(rng):
    d = base(rng); lw = int(W).bit_length() - 1
    d["hue"] = np.minimum((np.exp2(8 * rng.random((N, 8, 1, W))) * rng.random((N, 8, 16, W))).astype(np.int64), 255)
    n = np.minimum(np.exp2(lw * rng.random((N, 8, 16, B))).astype(np.int64) - 1, W - 1)
    d["own"] = np.where(rng.random((N, 8, 16, B)) < 0.5, W - 1 - n, n)
    for k in ("tau", "prev", "foe"): d[k] = np.minimum((B * rng.random((N, 8, B)) ** rng.choice(np.array([1.0, 2.0, 4.0]), (N, 8, 1))).astype(np.int64), B - 1)
    d["nb"] = np.minimum((B * rng.random((N, 8, 16, B)) ** 2).astype(np.int64), B - 1)
    d["tas"] = np.minimum((1024 * rng.random((N, 8, B)) ** 3).astype(np.int64), 1023)
    d["wt"] = np.minimum(np.exp2(8 * rng.random((N, 8, 16, 1))).astype(np.int64), 255)
    return pack(d)
def setup_inputs_ends(rng):
    d = base(rng)
    def pick(hi, *s): return hi * rng.integers(0, 2, s)
    d["hue"] = pick(255, N, 8, 16, W); o = pick(W - 1, N, 8, 16, B); kind = rng.integers(0, 4, (N, 8, 1, B))
    o = np.where(kind == 0, 0, np.where(kind == 1, W - 1, o)); u = pick(1023, N, 8, B); ta = pick(B - 1, N, 8, B)
    for k in ("prev", "foe"): d[k] = pick(B - 1, N, 8, B)
    d["foe"] = np.where(rng.random((N, 8, B)) < 0.3, rng.integers(0, B, (N, 8, B)), d["foe"])
    d["nb"] = pick(B - 1, N, 8, 16, B); w = pick(255, N, 8, 16, 1); w[:, 7] = 255; w[:, 3] = 0
    ca, cb, cc, cd = spot(W - 1, 0, 0), spot(W - 1, 1023, 0), spot(W - 2, 1023, 0), spot(W - 2, 0, 0)
    cnt = np.array([NEED - 1, NEED, NEED - 1, NEED - 1, NEED, NEED - 1, NEED - 1, NEED - 1])
    d["hue"][..., 0] = 0; d["hue"][..., cd] = 0; d["hue"][..., cb] = 255; d["hue"][..., cc] = 255; d["hue"][:, :, 5, cc] = 254
    d["hue"][..., ca] = np.where(np.argsort(rng.random((N, 8, 16)), axis=2) < cnt[None, :, None], 255, 0)
    for v, p in ((0, (2, 14)), (B - 1, (3, 15))):
        o[..., v] = 0; o[:, :, 1, v] = W - 2; o[:, :, p[0], v] = W - 1; o[:, :, p[1], v] = W - 1; u[..., v] = 0
    ta[..., 0] = 0; ta[..., 1] = B - 1; o[..., 1] = 0; u[..., 1] = 1023
    o[..., B - 2] = W - 1; u[..., B - 2] = 1023
    ta[N - 1, 7] = 0; ta[N - 1, 7, B - 1] = B - 1; o[N - 1, 7, :, B - 1] = 0; u[N - 1, 7, B - 1] = 1023
    d["own"], d["tas"], d["tau"], d["wt"] = o, u, ta, w
    return pack(d)
def check_inputs(d):
    bad = []
    for k, hi in (("hue", 255), ("own", W - 1), ("nb", B - 1), ("tau", B - 1), ("prev", B - 1), ("foe", B - 1), ("tas", 1023), ("wt", 255)):
        v = np.asarray(d[k]).astype(np.float64)
        if not (np.min(v) >= 0 and np.max(v) <= hi): bad.append("range of " + k)
        elif np.any(v != np.floor(v)): bad.append("whole numbers of " + k)
    return bad
def look(x, names, u, t):
    c = spot(names, u[:, None, :], t).reshape(8, 1, 16 * B)
    return np.take_along_axis(x, c, 2).reshape(8, 16, 16, B)
def reference(hue, own, nb, tau, prev, foe, tas, wt):
    x = hue.astype(np.float32).astype(np.int64).reshape(N, 8, 16, W); o = own.astype(np.int64).reshape(N, 8, 16, B); nx = nb.astype(np.int64).reshape(N, 8, 16, B)
    ta, pr, fo, u = tau.astype(np.int64), prev.astype(np.int64), foe.astype(np.int64), tas.astype(np.int64)
    w = wt.astype(np.int64).reshape(N, 8, 16, 1); bird = np.arange(B)[None, :]; grp = np.arange(8)[:, None]
    for t in range(RO):
        dist = 1 + t % (N - 1); top, low, raids = [], [], []
        for r in range(N):
            v = look(x[r], o[r], u[r], t); m = np.max(v, axis=2); top.append(m)
            low.append(np.argmin(np.add.reduce((v == m[:, :, None, :]).astype(np.int64), axis=1), axis=1))
        for r in range(N):
            q = (r + dist) % N; ix = ta[r][:, None, :]
            y = look(x[q], np.take_along_axis(o[q], ix, 2), u[r], t)
            g = np.argmax(np.add.reduce(np.maximum(y - top[r][:, :, None, :], 0), axis=1), axis=1)
            ok = np.add.reduce((np.take_along_axis(top[q], ix, 2) > top[r]).astype(np.int64), axis=1) < NEED
            first = np.full((8, B), B, np.int64); np.minimum.at(first, (np.broadcast_to(grp, (8, B)), ta[r]), np.where(ok, bird, B))
            a, b = np.nonzero(ok & (np.take_along_axis(first, ta[r], 1) == bird))
            raids.append((r, q, a, b, ta[r][a, b], g[a, b], low[r][a, b]))
        no, nt, npr, nf = np.array(o), np.array(fo), np.array(pr), np.array(fo); stolen = np.zeros((N, 1, 1), np.int64)
        for r, q, a, b, v, g, j in raids:
            no[r, a, j, b] = o[q, a, g, v]; npr[r, a, b] = v; nt[r, a, b] = nx[q, a, g, v]
        for r, q, a, b, v, g, j in raids:
            no[q, a, g, v] = o[r, a, j, b]; nf[q, a, v] = b; nt[q, a, v] = pr[r, a, b]; stolen[q] = len(a)
        u = (np.add.reduce(w * np.stack(top), axis=2) + stolen) & 1023
        o, ta, pr, fo = no, nt, npr, nf
    return {"yo": o.reshape(N, 128, B).astype(np.float32), "yt": ta.astype(np.float32), "yp": pr.astype(np.float32), "yf": fo.astype(np.float32), "yu": u.astype(np.float32)}

@@ -1,0 +1,533 @@
+from concourse.mybir import AluOpType as A, ActivationFunctionType as F
+
+NR, B, W, WX = 4, 256, 4096, 4336
+XS = 192
+SE, SY = [], list(range(6, 16))
+f4, b2, i4, u2 = "float32", "bfloat16", "int32", "uint16"
+SCRATCH = {}
+for _n, _c, _d in (
+        ("in8", 1024, i4), ("ownI", 256, i4), ("nbI", 256, i4), ("wtI", 8, i4), ("hueS", WX, b2), ("nbB", 256, b2),
+        ("ident", 128, b2), ("nident", 128, b2), ("BO", 128, b2), ("BO2", 256, b2), ("BO2T", 128, b2), ("Dm", 128, b2), ("Dtmp", 128, b2),
+        ("nBO16", 128, b2), ("B8p", 8, b2), ("B8n", 8, b2), ("WT", 128, b2), ("dmask", 256, b2), ("smask", 2048, b2), ("mask8", 128, b2),
+        ("kmask", 128, f4), ("Kc", 128, b2), ("BOf", 128, f4), ("nBOf", 128, f4), ("onesf", 128, f4), ("E8f", 128, f4), ("E8b", 128, b2),
+        ("identf", 128, f4), ("negone", 256, b2), ("SelU", 128, b2), ("lanep", 272, b2), ("clist", 16, u2), ("cols", 32, f4), ("colsI", 16, i4), ("iotA", 128, f4), ("iotB", 128, f4), ("iotC", 256, f4),
+        ("iotD", 256, f4), ("iotE", 128, f4), ("iotG", 128, f4), ("iotH", 16, f4), ("iotJ", 256, f4),
+        ("tasF", 256, f4), ("in8b", 768, b2),
+        ("mI", 256, i4), ("m2I", 256, i4), ("Hx", 256, u2), ("myI", 256, i4), ("my2I", 256, i4), ("Hy", 256, u2),
+        ("xg", 4096, b2), ("Rs", 4096, b2), ("Eb", 4096, b2), ("yg", 4096, b2), ("Yb", 4096, b2),
+        ("GE", 256, b2), ("LoT", 256, b2), ("thrHi", 256, b2), ("LoW", 256, b2), ("LoBig", 128, b2), ("LoWb", 256, b2), ("cmp", 256, b2),
+        ("OKHi", 256, b2), ("OK2w", 256, b2), ("Fm", 256, b2), ("Win", 256, b2), ("LvM", 128, b2), ("LvS", 128, b2), ("Lv", 16, u2), ("accW", 8, f4), ("cntS", 8, f4),
+        ("scE", 256, f4), ("keyE", 256, f4), ("ohE", 256, b2), ("scY", 256, f4), ("keyY", 256, f4), ("ohY", 256, b2),
+        ("MjS", 256, b2), ("MjW", 256, b2), ("gOj", 256, f4), ("Dj", 256, f4), ("MgS", 272, b2), ("t1", 256, f4), ("An", 256, f4), ("Bm", 256, b2),
+        ("Vt", 256, f4), ("NV", 256, b2), ("foeN", 256, b2), ("prevN", 256, b2), ("st", 256, b2), ("yst", 256, b2), ("mx", 256, b2), ("zz", 256, b2), ("Bt", 256, b2),
+        ("wp", 256, b2), ("wq", 256, b2), ("ee", 256, b2), ("dg", 256, b2), ("dgs", 256, b2), ("uI", 256, i4), ("suI", 256, i4),
+        ("outT", 1024, f4),
+        ("Own", 5 * 256, f4), ("foe1", 5 * 256, b2), ("TPs", 5 * 512, b2), ("Lts", 4 * 16, u2), ("u2S", 4 * 256, f4), ("Uc", 4 * 256, b2),
+        ("MjO", 4 * 256, f4), ("WinS", 4 * 256, b2), ("prV", 4 * 256, f4), ("prN", 4 * 256, b2),
+        ("TPl", 4 * 528, b2), ("Ltl", 4 * 16, u2), ("u2l", 4 * 256, f4), ("Ul", 4 * 256, b2), ("MjOl", 4 * 264, f4),
+        ("Winl", 4 * 256, b2), ("prVl", 4 * 256, f4), ("prNl", 4 * 256, b2)):
+    SCRATCH[_n] = ("sbuf", [128, _c], _d)
+for _i in range(8):
+    SCRATCH["ps%d" % _i] = ("psum", [128, 512], f4)
+KINDS = ("T", "P", "u", "U", "M", "w", "v", "n")
+SEMAPHORES = ["sv", "sa", "sp", "sg", "ls"] + ["d%d" % i for i in range(16)] + ["x%s%d" % (k, t) for k in KINDS for t in range(NR)]
+FILL = (8, 2, 2, 2, 2)
+PS = {"KE0": (0, 0, 128), "KY0": (0, 128, 128), "u2P": (0, 256, 256), "KE1": (1, 0, 128), "KY1": (1, 128, 128),
+      "D0": (3, 0, 512), "D1": (4, 0, 512), "Urep": (2, 0, 256), "Vrep": (2, 256, 256),
+      "loR": (3, 0, 256), "Ft": (3, 0, 256), "cntB": (3, 256, 256), "LvF": (3, 256, 128),
+      "HiB": (4, 0, 256), "Fn": (4, 0, 256), "foeQ": (6, 256, 256), "cnt": (4, 0, 1), "LoB": (4, 256, 256), "WinN": (4, 256, 256), "preQ": (7, 256, 256),
+      "St": (5, 0, 256), "OjV": (5, 0, 256), "nbg": (5, 0, 256), "MjT": (5, 256, 256), "MgT": (5, 256, 256),
+      "winR": (6, 0, 256), "foeP": (6, 256, 256), "tauP": (6, 0, 256), "Vg0": (7, 0, 128), "pr0": (7, 256, 128), "foeI": (7, 256, 256), "Vg1": (1, 256, 128), "pr1": (1, 384, 128)}
+
+
+def rank_program(g, core, T, topo):
+    rank = T.rank_of(core)
+    if rank is None:
+        return
+    qs = {"g": g, "v": g.vector, "a": g.scalar, "p": g.tensor, "s": g.sync}
+    esem = {"v": "sv", "a": "sa", "p": "sp", "g": "sg"}
+    cnt = {}
+    known = {q: {} for q in qs}
+    snap = {}
+    lastw, readers, bank = {}, {}, {}
+
+    def need(q, ev):
+        kn = known[q]
+        if kn.get(ev[0], 0) >= ev[1]:
+            return
+        qs[q].wait_ge(T.sem[ev[0]], ev[1])
+        for s, v in list(snap.get(ev, {}).items()) + [ev]:
+            if kn.get(s, 0) < v:
+                kn[s] = v
+
+    def deps(q, R, Wr):
+        for k in R:
+            w = lastw.get(k)
+            if w is not None and not (q == "p" and w[0] == "p"):
+                need(q, w[1])
+        for k in Wr:
+            w = lastw.get(k)
+            if w is not None and not (q == "p" and w[0] == "p"):
+                need(q, w[1])
+            for e, ev in readers.get(k, {}).items():
+                if e != q:
+                    need(q, ev)
+        for k in R + Wr:
+            if k in PS:
+                for e, ev in bank.get(PS[k][0], {}).items():
+                    if e != q:
+                        need(q, ev)
+
+    def note(q, ev, R, Wr):
+        snap[ev] = dict(known[q])
+        for k in R:
+            readers.setdefault(k, {})[q] = ev
+        for k in Wr:
+            lastw[k] = (q, ev)
+            readers[k] = {}
+        for k in R + Wr:
+            if k in PS:
+                bank.setdefault(PS[k][0], {})[q] = ev
+
+    def op(q, R, Wr, call):
+        R, Wr = R.split(), Wr.split()
+        deps(q, R, Wr)
+        ins = call(qs[q])
+        s = esem[q]
+        cnt[s] = cnt.get(s, 0) + 1
+        ins.then_inc(T.sem[s], 1)
+        note(q, (s, cnt[s]), R, Wr)
+
+    def dma(q, sem, R, Wr, out, in_):
+        R, Wr = R.split(), Wr.split()
+        deps(q, R, Wr)
+        qs[q].dma_start(out=out, in_=in_).then_inc(T.sem[sem], 16)
+        cnt[sem] = 16
+        snap[(sem, 16)] = dict(known[q])
+        for k in Wr:
+            lastw[k] = ("dma", (sem, 16))
+            readers[k] = {}
+        for k in R:
+            readers.setdefault(k, {})[sem] = (sem, 16)
+
+    def send(kind, t, dst, R, out, in_):
+        deps("g", R.split(), [])
+        rid, pid = topo.addr(dst)[:2]
+        g.remote_dma(out, in_, T.sem["x%s%d" % (kind, t)], T.sem.ls, pid, rid, topo.mask(core, dst))
+        cnt["ls"] = cnt.get("ls", 0) + len(topo.engines(core, dst))
+
+    def expect(kind, t, src, key):
+        s = "x%s%d" % (kind, t)
+        cnt[s] = len(topo.engines(src, core))
+        lastw[key] = ("net", (s, cnt[s]))
+
+    def ps(k, a=0, n=None, step=1):
+        b, c, w = PS[k]
+        n = w if n is None else n
+        return T["ps%d" % b][:, c + a:c + a + n:step] if step > 1 else T["ps%d" % b][:, c + a:c + a + n]
+
+    def sl(k, t, w=256, a=0, n=None):
+        n = w if n is None else n
+        return T[k][:, t * w + a:t * w + a + n]
+
+    def tt(R, Wr, out, a, b, o, q="v"):
+        op(q, R, Wr, lambda e: e.tensor_tensor(out=out, in0=a, in1=b, op=o))
+
+    def ts(R, Wr, out, a, s1, o1, s2=None, o2=None):
+        if o2 is None:
+            op("v", R, Wr, lambda e: e.tensor_scalar(out=out, in0=a, scalar1=s1, scalar2=None, op0=o1))
+        else:
+            op("v", R, Wr, lambda e: e.tensor_scalar(out=out, in0=a, scalar1=s1, scalar2=s2, op0=o1, op1=o2))
+
+    def cp(R, Wr, out, a):
+        op("v", R, Wr, lambda e: e.tensor_copy(out=out, in_=a))
+
+    def act(R, Wr, out, a, scale=1.0, bias=0.0, func=None, acc=None):
+        op("a", R, Wr, lambda e: e.activation(out=out, in_=a, func=F.Copy if func is None else func, bias=bias, scale=scale, accum_out=acc))
+
+    def scan(R, Wr, out, d0, d1, o0, o1):
+        op("v", R, Wr, lambda e: e.tensor_tensor_scan(out=out, data0=d0, data1=d1, initial=0.0, op0=o0, op1=o1))
+
+    def mm(R, Wr, out, l, r, start=True, stop=True):
+        op("p", R, Wr, lambda e: e.matmul(out, l, r, start, stop))
+
+    def ms(Wr, ap, c):
+        op("v", "", Wr, lambda e: e.memset(ap, c))
+
+    def iota(Wr, ap, pattern, base, cm, small=True):
+        if small:
+            op("g", "", Wr, lambda e: e.iota(ap, pattern, base, cm, allow_small_or_imprecise_dtypes=True))
+        else:
+            op("g", "", Wr, lambda e: e.iota(ap, pattern, base, cm))
+
+    def peer(k):
+        return T.cores[(rank + k) % NR]
+
+    dist = [1 + t % 3 for t in range(NR)]
+    for t in range(NR):
+        th, vi = peer(-dist[t]), peer(dist[t])
+        for kind, src, key in (("T", th, "Ltl"), ("P", th, "TPl"), ("u", th, "u2l"), ("U", th, "Ul"), ("M", th, "MjOl"), ("w", vi, "Winl"), ("v", vi, "prVl"), ("n", vi, "prNl")):
+            expect(kind, t, src, "%s%d" % (key, t))
+
+    in8 = T.in8
+    dma("s", "d0", "", "in8a", in8[0:8, 0:256], T.tas[:])
+    dma("a", "d3", "", "in8b0", in8[0:8, 256:512], T.tau[:])
+    dma("s", "d1", "", "ownI", T.ownI[:], T.own[:])
+    dma("a", "d4", "", "in8b1", in8[0:8, 512:768], T.prev[:])
+    dma("s", "d2", "", "hueA", T.hueS[:, 0:W], T.hue[:])
+    dma("a", "d5", "", "in8b2", in8[0:8, 768:1024], T.foe[:])
+    dma("s", "d6", "", "hueB", T.hueS[:, W:WX], T.hue[:, 0:WX - W])
+    dma("s", "d7", "", "wtI", T.wtI[:, 0:1], T.wt[:])
+    dma("s", "d8", "", "nbI", T.nbI[:], T.nb[:])
+    C, CI = T.cols, T.colsI
+    iota("ci0", CI[:, 0:1], [[0, 1]], 0, 1, False)
+    iota("iA", T.iotA[:], [[1, 8], [0, 16]], 0, 0)
+    iota("iB", T.iotB[:], [[1, 128]], 0, 0)
+    iota("iC", T.iotC[:], [[0, 16], [1, 16]], 0, 0)
+    iota("iD", T.iotD[:], [[0, 32], [1, 8]], 0, 0)
+    iota("iE", T.iotE[:], [[1, 16], [16, 8]], 0, 0)
+    iota("iG", T.iotG[:], [[0, 8], [-1, 16]], 15, 0)
+    iota("iH", T.iotH[:], [[16, 16]], 15, 0)
+    iota("iJ", T.iotJ[:], [[1, 256]], 1, 0)
+    ts("ci0", "ci1", CI[:, 1:2], CI[:, 0:1], 4, A.arith_shift_right)
+    ts("ci0", "ci2", CI[:, 2:3], CI[:, 0:1], 15, A.bitwise_and)
+    ts("ci0", "ci3", CI[:, 3:4], CI[:, 0:1], 7, A.bitwise_and)
+    cp("ci0 ci1 ci2 ci3", "c0", C[:, 0:4], CI[:, 0:4])
+    p_, pdiv, pmod, pm8 = C[:, 0:1], C[:, 1:2], C[:, 2:3], C[:, 3:4]
+    ts("c0 iA", "E8f", T.E8f[:], T.iotA[:], p_, A.is_equal)
+    act("E8f", "E8b", T.E8b[:], T.E8f[:])
+    ts("c0 iB", "ident", T.ident[:], T.iotB[:], p_, A.is_equal)
+    act("ident", "nident", T.nident[:], T.ident[:], -1.0)
+    ms("smask", T.smask[:], 1.0)
+    ms("smask", T.smask[:, 0:2048:16], 0.0)
+    ts("c0 iC", "dmask", T.dmask[:], T.iotC[:], pmod, A.is_equal)
+    ts("c0 iA", "BO", T.BO[:], T.iotA[:], pdiv, A.is_equal)
+    cp("in8a", "tasF", T.tasF[0:8, :], in8[0:8, 0:256])
+    mm("E8f tasF", "winR", ps("winR"), T.E8f[0:8, :], T.tasF[0:8, :])
+    ts("winR", "u2P", ps("u2P"), ps("winR"), 2.0, A.mult, 33.0, A.add)
+    act("u2P", "u2S0", sl("u2S", 0), ps("u2P"))
+    send("u", 0, peer(dist[0]), "u2S0", sl("u2l", 0), sl("u2S", 0))
+    cp("ownI", "Own00 Own01", sl("Own", 0), T.ownI[:])
+    for j in range(3):
+        cp("in8b%d" % j, "inb%d" % j, T.in8b[0:8, 256 * j:256 * j + 256], in8[0:8, 256 + 256 * j:512 + 256 * j])
+    mm("E8b inb0", "tauP", ps("tauP"), T.E8b[0:8, :], T.in8b[0:8, 0:256])
+    mm("E8b inb1", "foeP", ps("foeP"), T.E8b[0:8, :], T.in8b[0:8, 256:512])
+    mm("E8b inb2", "foeI", ps("foeI"), T.E8b[0:8, :], T.in8b[0:8, 512:768])
+
+    def new_list(t):
+        tt("tauP dmask", "dg", T.dg[:], ps("tauP"), T.dmask[:], A.mult)
+        scan("dg smask", "dgs", T.dgs[:], T.smask[:, 0:256], T.dg[:], A.mult, A.add)
+        cp("dgs", "Lts%d" % t, sl("Lts", t, 16), T.dgs[:, 15:256:16])
+        send("T", t, peer(dist[t]), "Lts%d" % t, sl("Ltl", t, 16), sl("Lts", t, 16))
+
+    def home_offsets(t, h):
+        x = slice(128 * h, 128 * h + 128)
+        tt("Own%d%d u2P" % (t, h), "mI%d" % h, T.mI[:, x], sl("Own", t, 256, 128 * h, 128), ps("u2P", 128 * h, 128), A.mult)
+        ts("mI%d" % h, "m2I%d" % h, T.m2I[:, x], T.mI[:, x], 5, A.arith_shift_right, 4095, A.bitwise_and)
+        ts("m2I%d" % h, "Hx%d" % h, T.Hx[:, x], T.m2I[:, x], float(77 * t), A.add)
+    home_offsets(0, 0)
+    home_offsets(0, 1)
+    new_list(0)
+    act("foeP", "prev0", sl("TPs", 0, 512, 256, 256), ps("foeP"))
+    act("foeI", "foe0", sl("foe1", 0), ps("foeI"), 1.0, 1.0)
+    ts("c0", "c6", C[:, 6:7], pmod, 16.0, A.mult)
+    ts("c0", "c7", C[:, 7:8], pmod, -16.0, A.add)
+    ts("c0", "c4", C[:, 4:5], pmod, 0.0, A.is_equal, -1000.0, A.mult)
+    ts("c0", "c5", C[:, 5:6], p_, -1.0, A.add)
+    tt("c4 c5", "c8", C[:, 8:9], C[:, 4:5], C[:, 5:6], A.add)
+    ts("c0", "c9", C[:, 9:10], p_, -256.0, A.add)
+    ts("c0", "c10", C[:, 10:11], p_, -128.0, A.add)
+    ts("c0", "c13", C[:, 13:14], p_, -1.1, A.mult, 62.0, A.add)
+    act("c13", "c11", C[:, 11:12], C[:, 13:14], 1.0, 0.0, F.Exp)
+    ts("c11", "c12", C[:, 12:13], C[:, 11:12], 2.0, A.mult)
+    act("BO", "nBO16", T.nBO16[:], T.BO[:], -16.0)
+    act("BO", "BOf", T.BOf[:], T.BO[:])
+    act("BO", "nBOf", T.nBOf[:], T.BO[:], -1.0)
+    act("BO", "B8p", T.B8p[:], T.BO[:, 0:128:16], 16.0)
+    act("BO", "B8n", T.B8n[:], T.BO[:, 0:128:16], -16.0)
+    act("iG", "Kc", T.Kc[:], T.iotG[:])
+    ts("c0 iE", "Dm", T.Dm[:], T.iotE[:], p_, A.is_equal)
+    ts("c8 iE", "Dtmp", T.Dtmp[:], T.iotE[:], C[:, 8:9], A.is_equal)
+    tt("Dm Dtmp", "Dm", T.Dm[:], T.Dm[:], T.Dtmp[:], A.subtract)
+    act("iJ", "lanep1", T.lanep[:, 0:256], T.iotJ[:])
+
+    def mid_constants():
+        cp("wtI", "c14", C[:, 14:15], T.wtI[:, 0:1])
+        ts("BO c14", "WT", T.WT[:], T.BO[:], C[:, 14:15], A.mult)
+        cp("nbI", "nbB", T.nbB[:], T.nbI[:])
+        ts("c0 iD", "BO2", T.BO2[:], T.iotD[:], pdiv, A.is_equal)
+        for t in range(NR):
+            ms("TPz", T.TPl[:, 528 * t + 512:528 * t + 528], 0.0)
+            ms("MjOz", T.MjOl[:, 264 * t + 256:264 * t + 264], 0.0)
+        ms("lanep", T.lanep[:, 256:272], 0.0)
+        ts("iD", "mask8", T.mask8[:], T.iotD[:, 0:128], 0.0, A.is_gt)
+
+    def late_constants():
+        ms("onesf", T.onesf[:], 1.0)
+        ms("kmask", T.kmask[:], 0.0)
+        ms("kmask", T.kmask[:, 0:128:16], -1048576.0)
+        cp("iH", "clist", T.clist[:], T.iotH[:])
+        ts("c0 iA", "BO2T", T.BO2T[:], T.iotA[:], pm8, A.is_equal)
+        ts("iG", "SelU", T.SelU[:], T.iotG[:], 15.0 - min(SY + [15]), A.is_le, 16.0, A.mult)
+        tt("SelU BO", "SelU", T.SelU[:], T.SelU[:], T.BO[:], A.mult)
+        ms("MgS", T.MgS[:], 0.0)
+        ms("negone", T.negone[:], -1.0)
+
+    HU = T.hueS[:, 0:WX]
+
+    for t in range(NR):
+        last = t == NR - 1
+        thief, victim = peer(-dist[t]), peer(dist[t])
+        Ot, Ut, Lt = sl("Own", t), sl("Uc", t), sl("Ltl", t, 16)
+        own, uc, ltl, tpl = "Own%d0 Own%d1" % (t, t), "Uc%d" % t, "Ltl%d" % t, "TPl%d" % t
+        tau = T.TPl[:, 528 * t:528 * t + 256]
+        I, nI = T.ident[:], T.nident[:]
+        act("hueA hueB Hx0", "xgA", T.xg[:, 0:2048], HU.indirect(T.Hx[:, 0:128]))
+        act("tauP", "tau%d" % t, sl("TPs", t, 512, 0, 256), ps("tauP"))
+        if t:
+            act("preQ", "prev%d" % t, sl("TPs", t, 512, 256, 256), ps("preQ"))
+        send("P", t, victim, "tau%d prev%d" % (t, t), T.TPl[:, 528 * t:528 * t + 512], sl("TPs", t, 512))
+        act("hueA hueB Hx1", "xgB", T.xg[:, 2048:16 * XS], HU.indirect(T.Hx[:, 128:XS]))
+        cp("hueA hueB Hx1", "xgV", T.xg[:, 16 * XS:4096], HU.indirect(T.Hx[:, XS:256]))
+        if t == 0:
+            mid_constants()
+        scan("xgA smask", "RsA", T.Rs[:, 0:2048], T.smask[:, 0:2048], T.xg[:, 0:2048], A.mult, A.max)
+        tt("%s %s u2l%d" % (own, ltl, t), "myI", T.myI[:], Ot.indirect(Lt), sl("u2l", t), A.mult)
+        ts("myI", "my2I", T.my2I[:], T.myI[:], 5, A.arith_shift_right, 4095, A.bitwise_and)
+        ts("my2I", "Hy", T.Hy[:], T.my2I[:], float(77 * t), A.add)
+        act("hueA hueB Hy", "yg0", T.yg[:, 0:2048], HU.indirect(T.Hy[:, 0:128]))
+        scan("xgV smask", "RsV", T.Rs[:, 16 * XS:4096], T.smask[:, 0:4096 - 16 * XS], T.xg[:, 16 * XS:4096], A.mult, A.max)
+        ts("%s c6" % tpl, "GE", T.GE[:], tau, C[:, 6:7], A.is_ge)
+        mm("ident %s" % tpl, "loR", ps("loR"), I, tau, True, False)
+        mm("nBO16 GE", "loR", ps("loR"), T.nBO16[:], T.GE[:], False, True)
+        for h in range(2):
+            mm("GE Dm", "HiB", ps("HiB", 128 * h, 128), T.GE[:, 128 * h:128 * h + 128], T.Dm[:])
+        scan("xgB smask", "RsB", T.Rs[:, 2048:16 * XS], T.smask[:, 0:16 * XS - 2048], T.xg[:, 2048:16 * XS], A.mult, A.max)
+        cp("RsV RsA RsB", uc, Ut, T.Rs[:, 15:4096:16])
+        send("U", t, victim, uc, sl("Ul", t), Ut)
+        mm("ident %s" % uc, "Urep", ps("Urep"), I, Ut)
+        ts("loR c7", "LoT", T.LoT[:], ps("loR"), C[:, 7:8], A.is_equal)
+        for h in range(2):
+            mm("ident Kc", "KE%d" % h, ps("KE%d" % h), I, T.Kc[:, 0:128], True, False)
+        for h in range(2):
+            mm("LoT ident", "LoB", ps("LoB", 128 * h, 128), T.LoT[:, 128 * h:128 * h + 128], I)
+        mm("WT %s" % uc, "St", ps("St"), T.WT[:], Ut)
+        if t:
+            act("foeQ", "foe%d" % t, sl("foe1", t), ps("foeQ"))
+        act("HiB", "thrHi", T.thrHi[:], ps("HiB"), 9.0)
+        act("LoB c11", "LoW", T.LoW[:], ps("LoB"), C[:, 11:12])
+        act("LoB", "LoBig", T.LoBig[:], ps("LoB", 0, 128), float(2.0 ** 93))
+        act("LoB c9", "LoWb0", T.LoWb[:, 0:128], ps("LoB", 0, 128), C[:, 9:10])
+        act("LoB c10", "LoWb1", T.LoWb[:, 128:256], ps("LoB", 128, 128), C[:, 10:11])
+        act("hueA hueB Hy", "yg1", T.yg[:, 2048:4096], HU.indirect(T.Hy[:, 128:256]))
+        act("%s %s" % (own, ltl), "Vt", T.Vt[:], Ot.indirect(Lt))
+        act("nbB %s" % ltl, "NV", T.NV[:], T.nbB[:].indirect(Lt))
+
+        def diff(pair, j, X, Xk, neg, negk, bias, out, outk):
+            for i, k in enumerate(pair):
+                o = ps("D%d" % (j % 2), 256 * i, 256)
+                mm("ident " + Xk, "D%d" % (j % 2), o, I, X[:, k:4096:16], True, False)
+                mm("nident " + negk, "D%d" % (j % 2), o, nI, neg, False, True)
+            k = pair[0]
+            act("D%d" % (j % 2), "%s%d %s%d" % (outk, k, outk, k + 1), out[:, 256 * k:256 * k + 512], ps("D%d" % (j % 2)), 1.0, bias, F.Relu)
+
+        EV, YV = [k for k in range(16) if k not in SE], [k for k in range(16) if k not in SY]
+        todo = [("E", k) for k in EV] + [("Y", k) for k in YV]
+        wait_sums, left, opened = [], {"E": 16, "Y": 16}, []
+
+        def sums(what, k):
+            left[what] -= 1
+            K, M = ("KE", T.B8n) if what == "E" else ("KY", T.B8p)
+            buf = T.Eb if what == "E" else T.Yb
+            for h in range(2):
+                mm("%sb%d %s" % (what, k, "B8n" if what == "E" else "B8p"), "%s%d" % (K, h), ps("%s%d" % (K, h), k, 128 - k, 16),
+                   buf[:, 256 * k + 128 * h:256 * k + 128 * h + 128], M[:], False, left[what] == 0)
+
+        def ysum(k):
+            if opened:
+                sums("Y", k)
+            else:
+                wait_sums.append(k)
+
+        def fill(n):
+            for _ in range(n):
+                if not todo:
+                    return
+                what, k = todo.pop(0)
+                if what == "E":
+                    tt("xgV xgA xgB Urep", "Eb%d" % k, T.Eb[:, 256 * k:256 * k + 256], T.xg[:, k:4096:16], ps("Urep"), A.is_equal)
+                    sums("E", k)
+                else:
+                    tt("yg0 yg1 Vrep", "Yb%d" % k, T.Yb[:, 256 * k:256 * k + 256], T.yg[:, k:4096:16], ps("Vrep"), A.max)
+                    ysum(k)
+
+        dtodo = [("E", SE[i:i + 2]) for i in range(0, len(SE), 2)] + [("Y", SY[i:i + 2]) for i in range(0, len(SY), 2)]
+        dn = [0]
+
+        lag = []
+
+        def flush():
+            while lag:
+                what, k = lag.pop(0)
+                if what == "E":
+                    sums("E", k)
+                else:
+                    ysum(k)
+
+        def dfill(n):
+            for _ in range(n):
+                if not dtodo:
+                    return
+                what, pair = dtodo.pop(0)
+                if what == "E":
+                    diff(pair, dn[0], T.xg, "xgV xgA xgB", Ut, uc, 1.0, T.Eb, "Eb")
+                else:
+                    diff(pair, dn[0], T.yg, "yg0 yg1", sl("Ul", t), "Ul%d" % t, 0.0, T.Yb, "Yb")
+                flush()
+                lag.extend((what, k) for k in pair)
+                dn[0] += 1
+
+        if t == 0:
+            late_constants()
+        fill(FILL[0])
+        tt("%s %s Ul%d" % (uc, ltl, t), "cmp", T.cmp[:], Ut.indirect(Lt), sl("Ul", t), A.is_gt)
+        for h in range(2):
+            mm("cmp BO2", "cntB", ps("cntB", 128 * h, 128), T.cmp[:, 128 * h:128 * h + 128], T.BO2[:, 0:128])
+        mm("ident Ul%d" % t, "Vrep", ps("Vrep"), I, sl("Ul", t))
+        fill(FILL[1])
+        tt("cntB thrHi", "OKHi", T.OKHi[:], ps("cntB"), T.thrHi[:], A.is_lt)
+        mm("LoW OKHi", "Ft", ps("Ft", 0, 128), T.LoW[:, 0:128], T.OKHi[:, 0:128])
+        mm("LoBig OKHi", "Ft", ps("Ft", 128, 128), T.LoBig[:], T.OKHi[:, 0:128], True, False)
+        mm("LoW OKHi", "Ft", ps("Ft", 128, 128), T.LoW[:, 128:256], T.OKHi[:, 128:256], False, True)
+        ts("OKHi c12", "OK2w", T.OK2w[:], T.OKHi[:], C[:, 12:13], A.mult)
+        fill(FILL[2])
+        tt("Ft BO2", "Fm", T.Fm[:], ps("Ft"), T.BO2[:], A.mult)
+        for h in range(2):
+            mm("LoT Fm", "Fn", ps("Fn", 128 * h, 128), T.LoT[:, 128 * h:128 * h + 128], T.Fm[:, 128 * h:128 * h + 128])
+        fill(FILL[3])
+        tt("Fn OK2w", "Win", T.Win[:], ps("Fn"), T.OK2w[:], A.is_lt)
+        for h in range(2):
+            mm("LoWb%d Win" % h, "LvF", ps("LvF"), T.LoWb[:, 128 * h:128 * h + 128], T.Win[:, 128 * h:128 * h + 128], h == 0, h == 1)
+        for h in range(2):
+            mm("Win ident", "WinN", ps("WinN", 128 * h, 128), T.Win[:, 128 * h:128 * h + 128], T.ident[:])
+        act("WinN", "WinS%d accW" % t, sl("WinS", t), ps("WinN"), acc=T.accW[:, 0:1])
+        send("w", t, thief, "WinS%d" % t, sl("Winl", t), sl("WinS", t))
+        mm("onesf accW", "cnt", ps("cnt"), T.onesf[:], T.accW[:, 0:1])
+        fill(FILL[4])
+        tt("LvF BO2", "LvM", T.LvM[:], ps("LvF"), T.BO2[:, 0:128], A.mult)
+        scan("LvM mask8", "LvS", T.LvS[:], T.mask8[:], T.LvM[:], A.mult, A.add)
+        ts("LvS", "Lv", T.Lv[:], T.LvS[:, 7:128:8], 256.0, A.add)
+        act("lanep lanep1 Lv", "foeN", T.foeN[:], T.lanep[:].indirect(T.Lv[:]))
+        act("foeN", "st", T.st[:], T.foeN[:], func=F.Sign)
+        act("%s TPz Lv" % tpl, "prevN", T.prevN[:], T.TPl[:, 528 * t + 256:528 * t + 528].indirect(T.Lv[:]))
+        cp("cnt", "cntS", T.cntS[:, 0:1], ps("cnt"))
+        while [x for x in todo if x[0] == "E"] or [x for x in dtodo if x[0] == "E"]:
+            dfill(1)
+            fill(2)
+        if SE:
+            flush()
+        ts("St cntS", "suI", T.suI[:], ps("St"), T.cntS[:, 0:1], A.add)
+        ts("suI", "uI", T.uI[:], T.suI[:], 1023, A.bitwise_and)
+
+        def best(e):
+            for h in range(2):
+                x, y = slice(128 * h, 128 * h + 128), slice(128 - 128 * h, 256 - 128 * h)
+                act("K%s%d" % (e, h), "key%s%d" % (e, h), T["key" + e][:, x], ps("K%s%d" % (e, h)))
+                scan("K%s%d kmask" % (e, 1 - h), "sc%s%d" % (e, 1 - h), T["sc" + e][:, y], T.kmask[:, 0:128], ps("K%s%d" % (e, 1 - h)), A.add, A.max)
+            tt("sc%s0 sc%s1 key%s0 key%s1 clist" % (e, e, e, e), "oh" + e, T["oh" + e][:], T["sc" + e][:].indirect(T.clist[:]), T["key" + e][:], A.is_equal)
+        dfill(1)
+        best("E")
+        dfill(1)
+        for h in range(2):
+            mm("ident Kc", "KY%d" % h, ps("KY%d" % h), I, T.Kc[:, 0:128], True, False)
+            mm("Ul%d SelU" % t, "KY%d" % h, ps("KY%d" % h), T.Ul[:, 256 * t + 128 * h:256 * t + 128 * h + 128], T.SelU[:], False, False)
+        opened.append(1)
+        for h in range(2):
+            mm("ohE ident", "MjT", ps("MjT", 128 * h, 128), T.ohE[:, 128 * h:128 * h + 128], T.ident[:])
+        if not last:
+            ts("uI", "u2P", ps("u2P"), T.uI[:], 2.0, A.mult, 33.0, A.add)
+            act("u2P", "u2S%d" % (t + 1), sl("u2S", t + 1), ps("u2P"))
+            send("u", t + 1, peer(dist[t + 1]), "u2S%d" % (t + 1), sl("u2l", t + 1), sl("u2S", t + 1))
+        else:
+            cp("uI", "outU", T.outT[:, 768:1024], T.uI[:])
+            dma("s", "d9", "outU", "yu", T.yu[:], T.outT[0:128:16, 768:1024])
+        for k in wait_sums:
+            sums("Y", k)
+        dfill(1)
+        tt("MjT %s" % own, "MjO%d" % t, sl("MjO", t), ps("MjT"), Ot, A.mult)
+        send("M", t, victim, "MjO%d" % t, T.MjOl[:, 264 * t:264 * t + 256], sl("MjO", t))
+        act("MjT", "MjS", T.MjS[:], ps("MjT"))
+        fill(1)
+        mm("BO2T Winl%d" % t, "winR", ps("winR"), T.BO2T[:], sl("Winl", t))
+        f1 = sl("foe1", t)
+        pv, ta = sl("TPs", t, 512, 256, 256), sl("TPs", t, 512, 0, 256)
+        mm("ident foe%d" % t, "foeP", ps("foeP"), T.ident[:], f1)
+        dfill(2)
+        fill(1)
+        tt("winR st", "mx", T.mx[:], ps("winR"), T.st[:], A.max)
+        tt("winR st", "Bt", T.Bt[:], ps("winR"), T.st[:], A.is_gt)
+        tt("winR MjS", "MjW", T.MjW[:], ps("winR"), T.MjS[:], A.mult)
+        tt("winR prev%d" % t, "wp", T.wp[:], ps("winR"), pv, A.mult)
+        tt("winR tau%d" % t, "wq", T.wq[:], ps("winR"), ta, A.mult)
+        tt("foeP st", "yst", T.yst[:], ps("foeP"), T.st[:], A.mult)
+        tt("foeP mx", "zz", T.zz[:], ps("foeP"), T.mx[:], A.mult)
+        while todo or dtodo:
+            dfill(1)
+            fill(2)
+        flush()
+        act("MjOl%d MjOz Lv" % t, "gOj", T.gOj[:], T.MjOl[:, 264 * t:264 * t + 264].indirect(T.Lv[:]))
+        mm("BOf gOj", "OjV", ps("OjV"), T.BOf[:], T.gOj[:])
+        best("Y")
+        for h in range(2):
+            mm("ohY ident", "MgT", ps("MgT", 128 * h, 128), T.ohY[:, 128 * h:128 * h + 128], T.ident[:])
+        tt("MgT Vt", "prV%d" % t, sl("prV", t), ps("MgT"), T.Vt[:], A.mult)
+        send("v", t, thief, "prV%d" % t, sl("prVl", t), sl("prV", t))
+        tt("MgT NV", "prN%d" % t, sl("prN", t), ps("MgT"), T.NV[:], A.mult)
+        send("n", t, thief, "prN%d" % t, sl("prNl", t), sl("prN", t))
+        act("MgT", "MgS", T.MgS[:, 0:256], ps("MgT"))
+        tt("OjV %s" % own, "Dj", T.Dj[:], ps("OjV"), Ot, A.subtract)
+        tt("MgS Lv Dj", "t1", T.t1[:], T.MgS[:].indirect(T.Lv[:]), T.Dj[:], A.mult)
+        tt("MgS Lv MjW", "Bm", T.Bm[:], T.MgS[:].indirect(T.Lv[:]), T.MjW[:], A.is_lt)
+        tt("t1 %s" % own, "An", T.An[:], T.t1[:], Ot, A.add)
+
+        def prev_foe():
+            mm("ident prev%d" % t, "preQ", ps("preQ"), I, pv, True, False)
+            mm("nident wp", "preQ", ps("preQ"), nI, T.wp[:], False, False)
+            mm("ident wq", "preQ", ps("preQ"), I, T.wq[:], False, True)
+            mm("ident foe%d" % t, "foeQ", ps("foeQ"), I, f1, True, False)
+            mm("nident yst", "foeQ", ps("foeQ"), nI, T.yst[:], False, False)
+            mm("ident foeN", "foeQ", ps("foeQ"), I, T.foeN[:], False, True)
+        if last:
+            prev_foe()
+            act("foeQ", "outF", T.outT[:, 512:768], ps("foeQ"), 1.0, -1.0)
+            act("preQ", "outP", T.outT[:, 256:512], ps("preQ"))
+            dma("s", "d10", "outF", "yf", T.yf[:], T.outT[0:128:16, 512:768])
+            dma("s", "d11", "outP", "yp", T.yp[:], T.outT[0:128:16, 256:512])
+        for h in range(2):
+            mm("nBOf MjO%d" % t, "Vg%d" % h, ps("Vg%d" % h), T.nBOf[:], sl("MjO", t, 256, 128 * h, 128), True, False)
+        mm("ident prevN", "tauP", ps("tauP"), I, T.prevN[:], True, False)
+        mm("ident foe%d" % t, "tauP", ps("tauP"), I, f1, False, False)
+        mm("nident zz", "tauP", ps("tauP"), nI, T.zz[:], False, False)
+        mm("ident mx", "tauP", ps("tauP"), I, T.mx[:], False, False)
+        mm("ident negone", "tauP", ps("tauP"), I, T.negone[:], False, False)
+        for h in range(2):
+            mm("BOf prVl%d" % t, "Vg%d" % h, ps("Vg%d" % h), T.BOf[:], sl("prVl", t, 256, 128 * h, 128), False, True)
+        mm("BO prNl%d" % t, "nbg", ps("nbg"), T.BO[:], sl("prNl", t))
+        for h in range(2):
+            x = slice(128 * h, 128 * h + 128)
+            tt("Vg%d Bm" % h, "pr%d" % h, ps("pr%d" % h), ps("Vg%d" % h), T.Bm[:, x], A.mult)
+            tt("pr%d An" % h, "Own%d%d" % (t + 1, h), sl("Own", t + 1, 256, 128 * h, 128), ps("pr%d" % h), T.An[:, x], A.add)
+            if not last:
+                home_offsets(t + 1, h)
+        if last:
+            dma("s", "d12", "Own40 Own41", "yo", T.yo[:], sl("Own", 4))
+        tt("nbg Bt", "ee", T.ee[:], ps("nbg"), T.Bt[:], A.mult)
+        mm("ident ee", "tauP", ps("tauP"), I, T.ee[:], False, True)
+        if not last:
+            new_list(t + 1)
+            prev_foe()
+        else:
+            act("tauP", "outTau", T.outT[:, 0:256], ps("tauP"))
+            dma("s", "d13", "outTau", "yt", T.yt[:], T.outT[0:128:16, 0:256])
+    for s in sorted(cnt):
+        need("s", (s, cnt[s]))

@@ -2,13 +2,13 @@ from concourse.mybir import AluOpType as A, ActivationFunctionType as F
 
 NR, B, W, WX = 4, 256, 4096, 4336
 XS = 192
-SE, SY = [], list(range(6, 16))
+SE, SY = [], list(range(8, 16))
 f4, b2, i4, u2 = "float32", "bfloat16", "int32", "uint16"
 SCRATCH = {}
 for _n, _c, _d in (
         ("in8", 1024, i4), ("ownI", 256, i4), ("nbI", 256, i4), ("wtI", 8, i4), ("hueS", WX, b2), ("nbB", 256, b2),
         ("ident", 128, b2), ("nident", 128, b2), ("BO", 128, b2), ("BO2", 256, b2), ("BO2T", 128, b2), ("Dm", 128, b2), ("Dtmp", 128, b2),
-        ("nBO16", 128, b2), ("B8p", 8, b2), ("B8n", 8, b2), ("WT", 128, b2), ("dmask", 256, b2), ("smask", 2048, b2), ("mask8", 128, b2),
+        ("nBO8", 128, b2), ("dW2", 128, b2), ("dd", 256, b2), ("nf", 256, b2), ("wd", 256, b2), ("B8p", 8, b2), ("B8n", 8, b2), ("WT", 128, b2), ("dmask", 256, b2), ("smask", 2048, b2), ("mask8", 128, b2),
         ("kmask", 128, f4), ("Kc", 128, b2), ("BOf", 128, f4), ("nBOf", 128, f4), ("onesf", 128, f4), ("E8f", 128, f4), ("E8b", 128, b2),
         ("identf", 128, f4), ("negone", 256, b2), ("SelU", 128, b2), ("lanep", 272, b2), ("clist", 16, u2), ("cols", 32, f4), ("colsI", 16, i4), ("iotA", 128, f4), ("iotB", 128, f4), ("iotC", 256, f4),
         ("iotD", 256, f4), ("iotE", 128, f4), ("iotG", 128, f4), ("iotH", 16, f4), ("iotJ", 256, f4),
@@ -19,8 +19,8 @@ for _n, _c, _d in (
         ("OKHi", 256, b2), ("OK2w", 256, b2), ("Fm", 256, b2), ("Win", 256, b2), ("LvM", 128, b2), ("LvS", 128, b2), ("Lv", 16, u2), ("accW", 8, f4), ("cntS", 8, f4),
         ("scE", 256, f4), ("keyE", 256, f4), ("ohE", 256, b2), ("scY", 256, f4), ("keyY", 256, f4), ("ohY", 256, b2),
         ("MjS", 256, b2), ("MjW", 256, b2), ("gOj", 256, f4), ("Dj", 256, f4), ("MgS", 272, b2), ("t1", 256, f4), ("An", 256, f4), ("Bm", 256, b2),
-        ("Vt", 256, f4), ("NV", 256, b2), ("foeN", 256, b2), ("prevN", 256, b2), ("st", 256, b2), ("yst", 256, b2), ("mx", 256, b2), ("zz", 256, b2), ("Bt", 256, b2),
-        ("wp", 256, b2), ("wq", 256, b2), ("ee", 256, b2), ("dg", 256, b2), ("dgs", 256, b2), ("uI", 256, i4), ("suI", 256, i4),
+        ("Vt", 256, f4), ("NV", 256, b2), ("foeN", 256, b2), ("prevN", 256, b2), ("nn", 256, b2), ("Bt", 256, b2),
+        ("ee", 256, b2), ("dg", 256, b2), ("dgs", 256, b2), ("uI", 256, i4), ("suI", 256, i4),
         ("outT", 1024, f4),
         ("Own", 5 * 256, f4), ("foe1", 5 * 256, b2), ("TPs", 5 * 512, b2), ("Lts", 4 * 16, u2), ("u2S", 4 * 256, f4), ("Uc", 4 * 256, b2),
         ("MjO", 4 * 256, f4), ("WinS", 4 * 256, b2), ("prV", 4 * 256, f4), ("prN", 4 * 256, b2),
@@ -31,12 +31,13 @@ for _i in range(8):
     SCRATCH["ps%d" % _i] = ("psum", [128, 512], f4)
 KINDS = ("T", "P", "u", "U", "M", "w", "v", "n")
 SEMAPHORES = ["sv", "sa", "sp", "sg", "ls"] + ["d%d" % i for i in range(16)] + ["x%s%d" % (k, t) for k in KINDS for t in range(NR)]
-FILL = (8, 2, 2, 2, 2)
+VF = (4, 3)
+FILL = (4, 3, 2, 2, 2, 3)
 PS = {"KE0": (0, 0, 128), "KY0": (0, 128, 128), "u2P": (0, 256, 256), "KE1": (1, 0, 128), "KY1": (1, 128, 128),
       "D0": (3, 0, 512), "D1": (4, 0, 512), "Urep": (2, 0, 256), "Vrep": (2, 256, 256),
       "loR": (3, 0, 256), "Ft": (3, 0, 256), "cntB": (3, 256, 256), "LvF": (3, 256, 128),
-      "HiB": (4, 0, 256), "Fn": (4, 0, 256), "foeQ": (6, 256, 256), "cnt": (4, 0, 1), "LoB": (4, 256, 256), "WinN": (4, 256, 256), "preQ": (7, 256, 256),
-      "St": (5, 0, 256), "OjV": (5, 0, 256), "nbg": (5, 0, 256), "MjT": (5, 256, 256), "MgT": (5, 256, 256),
+      "HiB": (4, 0, 256), "Fn": (4, 0, 256), "foeQ": (6, 256, 256), "cnt": (2, 0, 1), "LoB": (4, 256, 256), "WinN": (4, 256, 256), "preQ": (7, 256, 256),
+      "St": (5, 0, 256), "OjV": (7, 256, 256), "ddP": (7, 0, 256), "nbg": (5, 0, 256), "MjT": (5, 256, 256), "MgT": (5, 256, 256),
       "winR": (6, 0, 256), "foeP": (6, 256, 256), "tauP": (6, 0, 256), "Vg0": (7, 0, 128), "pr0": (7, 256, 128), "foeI": (7, 256, 256), "Vg1": (1, 256, 128), "pr1": (1, 384, 128)}
 
 
@@ -230,8 +231,8 @@ def rank_program(g, core, T, topo):
     new_list(0)
     act("foeP", "prev0", sl("TPs", 0, 512, 256, 256), ps("foeP"))
     act("foeI", "foe0", sl("foe1", 0), ps("foeI"), 1.0, 1.0)
-    ts("c0", "c6", C[:, 6:7], pmod, 16.0, A.mult)
-    ts("c0", "c7", C[:, 7:8], pmod, -16.0, A.add)
+    ts("c0", "c6", C[:, 6:7], pmod, -16.0, A.mult, 0.5, A.add)
+    ts("c0", "c7", C[:, 7:8], pmod, 112.0, A.add)
     ts("c0", "c4", C[:, 4:5], pmod, 0.0, A.is_equal, -1000.0, A.mult)
     ts("c0", "c5", C[:, 5:6], p_, -1.0, A.add)
     tt("c4 c5", "c8", C[:, 8:9], C[:, 4:5], C[:, 5:6], A.add)
@@ -239,8 +240,9 @@ def rank_program(g, core, T, topo):
     ts("c0", "c10", C[:, 10:11], p_, -128.0, A.add)
     ts("c0", "c13", C[:, 13:14], p_, -1.1, A.mult, 62.0, A.add)
     act("c13", "c11", C[:, 11:12], C[:, 13:14], 1.0, 0.0, F.Exp)
-    ts("c11", "c12", C[:, 12:13], C[:, 11:12], 2.0, A.mult)
-    act("BO", "nBO16", T.nBO16[:], T.BO[:], -16.0)
+    ts("c11", "c12", C[:, 12:13], C[:, 11:12], -2.0, A.mult)
+    act("BO", "nBO8", T.nBO8[:], T.BO[:], -8.0)
+    act("ident c12", "dW2", T.dW2[:], T.ident[:], C[:, 12:13])
     act("BO", "BOf", T.BOf[:], T.BO[:])
     act("BO", "nBOf", T.nBOf[:], T.BO[:], -1.0)
     act("BO", "B8p", T.B8p[:], T.BO[:, 0:128:16], 16.0)
@@ -249,6 +251,7 @@ def rank_program(g, core, T, topo):
     ts("c0 iE", "Dm", T.Dm[:], T.iotE[:], p_, A.is_equal)
     ts("c8 iE", "Dtmp", T.Dtmp[:], T.iotE[:], C[:, 8:9], A.is_equal)
     tt("Dm Dtmp", "Dm", T.Dm[:], T.Dm[:], T.Dtmp[:], A.subtract)
+    ts("Dm", "Dm", T.Dm[:, 120:128], T.Dm[:, 120:128], 2.0, A.mult)
     act("iJ", "lanep1", T.lanep[:, 0:256], T.iotJ[:])
 
     def mid_constants():
@@ -295,33 +298,25 @@ def rank_program(g, core, T, topo):
         tt("%s %s u2l%d" % (own, ltl, t), "myI", T.myI[:], Ot.indirect(Lt), sl("u2l", t), A.mult)
         ts("myI", "my2I", T.my2I[:], T.myI[:], 5, A.arith_shift_right, 4095, A.bitwise_and)
         ts("my2I", "Hy", T.Hy[:], T.my2I[:], float(77 * t), A.add)
-        act("hueA hueB Hy", "yg0", T.yg[:, 0:2048], HU.indirect(T.Hy[:, 0:128]))
+        act("hueA hueB Hy", "yg0", T.yg[:, 0:1024], HU.indirect(T.Hy[:, 0:64]))
         scan("xgV smask", "RsV", T.Rs[:, 16 * XS:4096], T.smask[:, 0:4096 - 16 * XS], T.xg[:, 16 * XS:4096], A.mult, A.max)
-        ts("%s c6" % tpl, "GE", T.GE[:], tau, C[:, 6:7], A.is_ge)
-        mm("ident %s" % tpl, "loR", ps("loR"), I, tau, True, False)
-        mm("nBO16 GE", "loR", ps("loR"), T.nBO16[:], T.GE[:], False, True)
-        for h in range(2):
-            mm("GE Dm", "HiB", ps("HiB", 128 * h, 128), T.GE[:, 128 * h:128 * h + 128], T.Dm[:])
         scan("xgB smask", "RsB", T.Rs[:, 2048:16 * XS], T.smask[:, 0:16 * XS - 2048], T.xg[:, 2048:16 * XS], A.mult, A.max)
         cp("RsV RsA RsB", uc, Ut, T.Rs[:, 15:4096:16])
         send("U", t, victim, uc, sl("Ul", t), Ut)
         mm("ident %s" % uc, "Urep", ps("Urep"), I, Ut)
-        ts("loR c7", "LoT", T.LoT[:], ps("loR"), C[:, 7:8], A.is_equal)
         for h in range(2):
             mm("ident Kc", "KE%d" % h, ps("KE%d" % h), I, T.Kc[:, 0:128], True, False)
-        for h in range(2):
-            mm("LoT ident", "LoB", ps("LoB", 128 * h, 128), T.LoT[:, 128 * h:128 * h + 128], I)
         mm("WT %s" % uc, "St", ps("St"), T.WT[:], Ut)
-        if t:
-            act("foeQ", "foe%d" % t, sl("foe1", t), ps("foeQ"))
-        act("HiB", "thrHi", T.thrHi[:], ps("HiB"), 9.0)
-        act("LoB c11", "LoW", T.LoW[:], ps("LoB"), C[:, 11:12])
-        act("LoB", "LoBig", T.LoBig[:], ps("LoB", 0, 128), float(2.0 ** 93))
-        act("LoB c9", "LoWb0", T.LoWb[:, 0:128], ps("LoB", 0, 128), C[:, 9:10])
-        act("LoB c10", "LoWb1", T.LoWb[:, 128:256], ps("LoB", 128, 128), C[:, 10:11])
-        act("hueA hueB Hy", "yg1", T.yg[:, 2048:4096], HU.indirect(T.Hy[:, 128:256]))
-        act("%s %s" % (own, ltl), "Vt", T.Vt[:], Ot.indirect(Lt))
-        act("nbB %s" % ltl, "NV", T.NV[:], T.nbB[:].indirect(Lt))
+        act("%s c6" % tpl, "GE", T.GE[:], tau, 1.0, C[:, 6:7], F.Sign)
+        mm("ident %s" % tpl, "loR", ps("loR"), I, tau, True, False)
+        mm("nBO8 GE", "loR", ps("loR"), T.nBO8[:], T.GE[:], False, True)
+        for h in range(2):
+            mm("GE Dm", "HiB", ps("HiB", 128 * h, 128), T.GE[:, 128 * h:128 * h + 128], T.Dm[:])
+        act("hueA hueB Hy", "yg1", T.yg[:, 1024:2048], HU.indirect(T.Hy[:, 64:128]))
+        f1 = sl("foe1", t)
+        pv, ta = sl("TPs", t, 512, 256, 256), sl("TPs", t, 512, 0, 256)
+        mm("ident tau%d" % t, "ddP", ps("ddP"), I, ta, True, False)
+        mm("nident prev%d" % t, "ddP", ps("ddP"), nI, pv, False, True)
 
         def diff(pair, j, X, Xk, neg, negk, bias, out, outk):
             for i, k in enumerate(pair):
@@ -358,7 +353,7 @@ def rank_program(g, core, T, topo):
                     tt("xgV xgA xgB Urep", "Eb%d" % k, T.Eb[:, 256 * k:256 * k + 256], T.xg[:, k:4096:16], ps("Urep"), A.is_equal)
                     sums("E", k)
                 else:
-                    tt("yg0 yg1 Vrep", "Yb%d" % k, T.Yb[:, 256 * k:256 * k + 256], T.yg[:, k:4096:16], ps("Vrep"), A.max)
+                    tt("yg0 yg1 yg2 Vrep", "Yb%d" % k, T.Yb[:, 256 * k:256 * k + 256], T.yg[:, k:4096:16], ps("Vrep"), A.max)
                     ysum(k)
 
         dtodo = [("E", SE[i:i + 2]) for i in range(0, len(SE), 2)] + [("Y", SY[i:i + 2]) for i in range(0, len(SY), 2)]
@@ -382,7 +377,7 @@ def rank_program(g, core, T, topo):
                 if what == "E":
                     diff(pair, dn[0], T.xg, "xgV xgA xgB", Ut, uc, 1.0, T.Eb, "Eb")
                 else:
-                    diff(pair, dn[0], T.yg, "yg0 yg1", sl("Ul", t), "Ul%d" % t, 0.0, T.Yb, "Yb")
+                    diff(pair, dn[0], T.yg, "yg0 yg1 yg2", sl("Ul", t), "Ul%d" % t, 0.0, T.Yb, "Yb")
                 flush()
                 lag.extend((what, k) for k in pair)
                 dn[0] += 1
@@ -390,44 +385,48 @@ def rank_program(g, core, T, topo):
         if t == 0:
             late_constants()
         fill(FILL[0])
+        ts("loR c7", "LoT", T.LoT[:], ps("loR"), C[:, 7:8], A.is_equal)
+        for h in range(2):
+            mm("LoT ident", "LoB", ps("LoB", 128 * h, 128), T.LoT[:, 128 * h:128 * h + 128], I)
+        act("HiB", "thrHi", T.thrHi[:], ps("HiB"), 4.5)
+        act("LoB c11", "LoW", T.LoW[:], ps("LoB"), C[:, 11:12])
+        act("LoB", "LoBig", T.LoBig[:], ps("LoB", 0, 128), float(2.0 ** 93))
+        act("LoB c9", "LoWb0", T.LoWb[:, 0:128], ps("LoB", 0, 128), C[:, 9:10])
+        act("LoB c10", "LoWb1", T.LoWb[:, 128:256], ps("LoB", 128, 128), C[:, 10:11])
+        act("hueA hueB Hy", "yg2", T.yg[:, 2048:4096], HU.indirect(T.Hy[:, 128:256]))
+        fill(FILL[5])
         tt("%s %s Ul%d" % (uc, ltl, t), "cmp", T.cmp[:], Ut.indirect(Lt), sl("Ul", t), A.is_gt)
         for h in range(2):
             mm("cmp BO2", "cntB", ps("cntB", 128 * h, 128), T.cmp[:, 128 * h:128 * h + 128], T.BO2[:, 0:128])
-        mm("ident Ul%d" % t, "Vrep", ps("Vrep"), I, sl("Ul", t))
         fill(FILL[1])
         tt("cntB thrHi", "OKHi", T.OKHi[:], ps("cntB"), T.thrHi[:], A.is_lt)
         mm("LoW OKHi", "Ft", ps("Ft", 0, 128), T.LoW[:, 0:128], T.OKHi[:, 0:128])
         mm("LoBig OKHi", "Ft", ps("Ft", 128, 128), T.LoBig[:], T.OKHi[:, 0:128], True, False)
         mm("LoW OKHi", "Ft", ps("Ft", 128, 128), T.LoW[:, 128:256], T.OKHi[:, 128:256], False, True)
-        ts("OKHi c12", "OK2w", T.OK2w[:], T.OKHi[:], C[:, 12:13], A.mult)
         fill(FILL[2])
         tt("Ft BO2", "Fm", T.Fm[:], ps("Ft"), T.BO2[:], A.mult)
         for h in range(2):
-            mm("LoT Fm", "Fn", ps("Fn", 128 * h, 128), T.LoT[:, 128 * h:128 * h + 128], T.Fm[:, 128 * h:128 * h + 128])
+            mm("dW2 OKHi", "Fn", ps("Fn", 128 * h, 128), T.dW2[:], T.OKHi[:, 128 * h:128 * h + 128], True, False)
+            mm("LoT Fm", "Fn", ps("Fn", 128 * h, 128), T.LoT[:, 128 * h:128 * h + 128], T.Fm[:, 128 * h:128 * h + 128], False, True)
         fill(FILL[3])
-        tt("Fn OK2w", "Win", T.Win[:], ps("Fn"), T.OK2w[:], A.is_lt)
+        ts("Fn", "Win", T.Win[:], ps("Fn"), 0.0, A.is_lt)
         for h in range(2):
             mm("LoWb%d Win" % h, "LvF", ps("LvF"), T.LoWb[:, 128 * h:128 * h + 128], T.Win[:, 128 * h:128 * h + 128], h == 0, h == 1)
         for h in range(2):
             mm("Win ident", "WinN", ps("WinN", 128 * h, 128), T.Win[:, 128 * h:128 * h + 128], T.ident[:])
         act("WinN", "WinS%d accW" % t, sl("WinS", t), ps("WinN"), acc=T.accW[:, 0:1])
         send("w", t, thief, "WinS%d" % t, sl("Winl", t), sl("WinS", t))
-        mm("onesf accW", "cnt", ps("cnt"), T.onesf[:], T.accW[:, 0:1])
         fill(FILL[4])
         tt("LvF BO2", "LvM", T.LvM[:], ps("LvF"), T.BO2[:, 0:128], A.mult)
         scan("LvM mask8", "LvS", T.LvS[:], T.mask8[:], T.LvM[:], A.mult, A.add)
         ts("LvS", "Lv", T.Lv[:], T.LvS[:, 7:128:8], 256.0, A.add)
-        act("lanep lanep1 Lv", "foeN", T.foeN[:], T.lanep[:].indirect(T.Lv[:]))
-        act("foeN", "st", T.st[:], T.foeN[:], func=F.Sign)
-        act("%s TPz Lv" % tpl, "prevN", T.prevN[:], T.TPl[:, 528 * t + 256:528 * t + 528].indirect(T.Lv[:]))
-        cp("cnt", "cntS", T.cntS[:, 0:1], ps("cnt"))
         while [x for x in todo if x[0] == "E"] or [x for x in dtodo if x[0] == "E"]:
-            dfill(1)
+            if dtodo and dtodo[0][0] == "E":
+                dfill(1)
             fill(2)
         if SE:
             flush()
-        ts("St cntS", "suI", T.suI[:], ps("St"), T.cntS[:, 0:1], A.add)
-        ts("suI", "uI", T.uI[:], T.suI[:], 1023, A.bitwise_and)
+        mm("ident Ul%d" % t, "Vrep", ps("Vrep"), I, sl("Ul", t))
 
         def best(e):
             for h in range(2):
@@ -435,51 +434,48 @@ def rank_program(g, core, T, topo):
                 act("K%s%d" % (e, h), "key%s%d" % (e, h), T["key" + e][:, x], ps("K%s%d" % (e, h)))
                 scan("K%s%d kmask" % (e, 1 - h), "sc%s%d" % (e, 1 - h), T["sc" + e][:, y], T.kmask[:, 0:128], ps("K%s%d" % (e, 1 - h)), A.add, A.max)
             tt("sc%s0 sc%s1 key%s0 key%s1 clist" % (e, e, e, e), "oh" + e, T["oh" + e][:], T["sc" + e][:].indirect(T.clist[:]), T["key" + e][:], A.is_equal)
-        dfill(1)
         best("E")
+        act("lanep lanep1 Lv", "foeN", T.foeN[:], T.lanep[:].indirect(T.Lv[:]))
+        act("foeN", "nn", T.nn[:], T.foeN[:], -1.0, 1.0, F.Relu)
         dfill(1)
+        for h in range(2):
+            mm("ohE ident", "MjT", ps("MjT", 128 * h, 128), T.ohE[:, 128 * h:128 * h + 128], T.ident[:])
+        mm("onesf accW", "cnt", ps("cnt"), T.onesf[:], T.accW[:, 0:1])
+        if t:
+            act("foeQ", "foe%d" % t, f1, ps("foeQ"))
+        dfill(1)
+        act("ddP", "dd", T.dd[:], ps("ddP"))
+        act("%s TPz Lv" % tpl, "prevN", T.prevN[:], T.TPl[:, 528 * t + 256:528 * t + 528].indirect(T.Lv[:]))
+        mm("ident foe%d" % t, "foeP", ps("foeP"), I, f1)
         for h in range(2):
             mm("ident Kc", "KY%d" % h, ps("KY%d" % h), I, T.Kc[:, 0:128], True, False)
             mm("Ul%d SelU" % t, "KY%d" % h, ps("KY%d" % h), T.Ul[:, 256 * t + 128 * h:256 * t + 128 * h + 128], T.SelU[:], False, False)
         opened.append(1)
-        for h in range(2):
-            mm("ohE ident", "MjT", ps("MjT", 128 * h, 128), T.ohE[:, 128 * h:128 * h + 128], T.ident[:])
-        if not last:
-            ts("uI", "u2P", ps("u2P"), T.uI[:], 2.0, A.mult, 33.0, A.add)
-            act("u2P", "u2S%d" % (t + 1), sl("u2S", t + 1), ps("u2P"))
-            send("u", t + 1, peer(dist[t + 1]), "u2S%d" % (t + 1), sl("u2l", t + 1), sl("u2S", t + 1))
-        else:
-            cp("uI", "outU", T.outT[:, 768:1024], T.uI[:])
-            dma("s", "d9", "outU", "yu", T.yu[:], T.outT[0:128:16, 768:1024])
+        dfill(1)
         for k in wait_sums:
             sums("Y", k)
-        dfill(1)
         tt("MjT %s" % own, "MjO%d" % t, sl("MjO", t), ps("MjT"), Ot, A.mult)
         send("M", t, victim, "MjO%d" % t, T.MjOl[:, 264 * t:264 * t + 256], sl("MjO", t))
         act("MjT", "MjS", T.MjS[:], ps("MjT"))
-        fill(1)
+        fill(VF[0])
         mm("BO2T Winl%d" % t, "winR", ps("winR"), T.BO2T[:], sl("Winl", t))
-        f1 = sl("foe1", t)
-        pv, ta = sl("TPs", t, 512, 256, 256), sl("TPs", t, 512, 0, 256)
-        mm("ident foe%d" % t, "foeP", ps("foeP"), T.ident[:], f1)
-        dfill(2)
-        fill(1)
-        tt("winR st", "mx", T.mx[:], ps("winR"), T.st[:], A.max)
-        tt("winR st", "Bt", T.Bt[:], ps("winR"), T.st[:], A.is_gt)
+        act("%s %s" % (own, ltl), "Vt", T.Vt[:], Ot.indirect(Lt))
+        dfill(1)
+        act("nbB %s" % ltl, "NV", T.NV[:], T.nbB[:].indirect(Lt))
+        fill(VF[1])
+        tt("foeP nn", "nf", T.nf[:], ps("foeP"), T.nn[:], A.mult)
+        tt("winR nn", "Bt", T.Bt[:], ps("winR"), T.nn[:], A.mult)
+        tt("winR dd", "wd", T.wd[:], ps("winR"), T.dd[:], A.mult)
         tt("winR MjS", "MjW", T.MjW[:], ps("winR"), T.MjS[:], A.mult)
-        tt("winR prev%d" % t, "wp", T.wp[:], ps("winR"), pv, A.mult)
-        tt("winR tau%d" % t, "wq", T.wq[:], ps("winR"), ta, A.mult)
-        tt("foeP st", "yst", T.yst[:], ps("foeP"), T.st[:], A.mult)
-        tt("foeP mx", "zz", T.zz[:], ps("foeP"), T.mx[:], A.mult)
         while todo or dtodo:
             dfill(1)
             fill(2)
         flush()
-        act("MjOl%d MjOz Lv" % t, "gOj", T.gOj[:], T.MjOl[:, 264 * t:264 * t + 264].indirect(T.Lv[:]))
-        mm("BOf gOj", "OjV", ps("OjV"), T.BOf[:], T.gOj[:])
         best("Y")
+        act("MjOl%d MjOz Lv" % t, "gOj", T.gOj[:], T.MjOl[:, 264 * t:264 * t + 264].indirect(T.Lv[:]))
         for h in range(2):
             mm("ohY ident", "MgT", ps("MgT", 128 * h, 128), T.ohY[:, 128 * h:128 * h + 128], T.ident[:])
+        mm("BOf gOj", "OjV", ps("OjV"), T.BOf[:], T.gOj[:])
         tt("MgT Vt", "prV%d" % t, sl("prV", t), ps("MgT"), T.Vt[:], A.mult)
         send("v", t, thief, "prV%d" % t, sl("prVl", t), sl("prV", t))
         tt("MgT NV", "prN%d" % t, sl("prN", t), ps("MgT"), T.NV[:], A.mult)
@@ -489,13 +485,21 @@ def rank_program(g, core, T, topo):
         tt("MgS Lv Dj", "t1", T.t1[:], T.MgS[:].indirect(T.Lv[:]), T.Dj[:], A.mult)
         tt("MgS Lv MjW", "Bm", T.Bm[:], T.MgS[:].indirect(T.Lv[:]), T.MjW[:], A.is_lt)
         tt("t1 %s" % own, "An", T.An[:], T.t1[:], Ot, A.add)
+        cp("cnt", "cntS", T.cntS[:, 0:1], ps("cnt"))
+        ts("St cntS", "suI", T.suI[:], ps("St"), T.cntS[:, 0:1], A.add)
+        ts("suI", "uI", T.uI[:], T.suI[:], 1023, A.bitwise_and)
+        if not last:
+            ts("uI", "u2P", ps("u2P"), T.uI[:], 2.0, A.mult, 33.0, A.add)
+            act("u2P", "u2S%d" % (t + 1), sl("u2S", t + 1), ps("u2P"))
+            send("u", t + 1, peer(dist[t + 1]), "u2S%d" % (t + 1), sl("u2l", t + 1), sl("u2S", t + 1))
+        else:
+            cp("uI", "outU", T.outT[:, 768:1024], T.uI[:])
+            dma("s", "d9", "outU", "yu", T.yu[:], T.outT[0:128:16, 768:1024])
 
         def prev_foe():
             mm("ident prev%d" % t, "preQ", ps("preQ"), I, pv, True, False)
-            mm("nident wp", "preQ", ps("preQ"), nI, T.wp[:], False, False)
-            mm("ident wq", "preQ", ps("preQ"), I, T.wq[:], False, True)
-            mm("ident foe%d" % t, "foeQ", ps("foeQ"), I, f1, True, False)
-            mm("nident yst", "foeQ", ps("foeQ"), nI, T.yst[:], False, False)
+            mm("ident wd", "preQ", ps("preQ"), I, T.wd[:], False, True)
+            mm("ident nf", "foeQ", ps("foeQ"), I, T.nf[:], True, False)
             mm("ident foeN", "foeQ", ps("foeQ"), I, T.foeN[:], False, True)
         if last:
             prev_foe()
@@ -506,13 +510,13 @@ def rank_program(g, core, T, topo):
         for h in range(2):
             mm("nBOf MjO%d" % t, "Vg%d" % h, ps("Vg%d" % h), T.nBOf[:], sl("MjO", t, 256, 128 * h, 128), True, False)
         mm("ident prevN", "tauP", ps("tauP"), I, T.prevN[:], True, False)
-        mm("ident foe%d" % t, "tauP", ps("tauP"), I, f1, False, False)
-        mm("nident zz", "tauP", ps("tauP"), nI, T.zz[:], False, False)
-        mm("ident mx", "tauP", ps("tauP"), I, T.mx[:], False, False)
-        mm("ident negone", "tauP", ps("tauP"), I, T.negone[:], False, False)
+        mm("ident nf", "tauP", ps("tauP"), I, T.nf[:], False, False)
+        mm("nident nn", "tauP", ps("tauP"), nI, T.nn[:], False, False)
+        mm("nident foe%d" % t, "nbg", ps("nbg"), nI, f1, True, False)
+        mm("nident negone", "nbg", ps("nbg"), nI, T.negone[:], False, False)
         for h in range(2):
             mm("BOf prVl%d" % t, "Vg%d" % h, ps("Vg%d" % h), T.BOf[:], sl("prVl", t, 256, 128 * h, 128), False, True)
-        mm("BO prNl%d" % t, "nbg", ps("nbg"), T.BO[:], sl("prNl", t))
+        mm("BO prNl%d" % t, "nbg", ps("nbg"), T.BO[:], sl("prNl", t), False, True)
         for h in range(2):
             x = slice(128 * h, 128 * h + 128)
             tt("Vg%d Bm" % h, "pr%d" % h, ps("pr%d" % h), ps("Vg%d" % h), T.Bm[:, x], A.mult)

from concourse.mybir import AluOpType as A, ActivationFunctionType as F

NR, B, W, WX = 4, 256, 4096, 4336
XS = 192
SE, SY = [], list(range(8, 16))
f4, b2, i4, u2 = "float32", "bfloat16", "int32", "uint16"
SCRATCH = {}
for _n, _c, _d in (
        ("in8", 1024, i4), ("ownI", 256, i4), ("nbI", 256, i4), ("wtI", 8, i4), ("hueS", WX, b2), ("nbB", 256, b2),
        ("ident", 128, b2), ("nident", 128, b2), ("BO", 128, b2), ("BO2", 256, b2), ("BO2T", 128, b2), ("Dm", 128, b2), ("Dtmp", 128, b2),
        ("nBO8", 128, b2), ("dW2", 128, b2), ("dd", 256, b2), ("nf", 256, b2), ("wd", 256, b2), ("B8p", 8, b2), ("B8n", 8, b2), ("WT", 128, b2), ("dmask", 256, b2), ("smask", 2048, b2), ("mask8", 128, b2),
        ("kmask", 128, f4), ("Kc", 128, b2), ("BOf", 128, f4), ("nBOf", 128, f4), ("onesf", 128, f4), ("E8f", 128, f4), ("E8b", 128, b2),
        ("identf", 128, f4), ("negone", 256, b2), ("SelU", 128, b2), ("lanep", 272, b2), ("clist", 16, u2), ("cols", 32, f4), ("colsI", 16, i4), ("iotA", 128, f4), ("iotB", 128, f4), ("iotC", 256, f4),
        ("iotD", 256, f4), ("iotE", 128, f4), ("iotG", 128, f4), ("iotH", 16, f4), ("iotJ", 256, f4),
        ("tasF", 256, f4), ("in8b", 768, b2),
        ("mI", 256, i4), ("m2I", 256, i4), ("Hx", 256, u2), ("myI", 256, i4), ("my2I", 256, i4), ("Hy", 256, u2),
        ("xg", 4096, b2), ("Rs", 4096, b2), ("Eb", 4096, b2), ("yg", 4096, b2), ("Yb", 4096, b2),
        ("GE", 256, b2), ("LoT", 256, b2), ("thrHi", 256, b2), ("LoW", 256, b2), ("LoBig", 128, b2), ("LoWb", 256, b2), ("cmp", 256, b2),
        ("OKHi", 256, b2), ("OK2w", 256, b2), ("Fm", 256, b2), ("Win", 256, b2), ("LvM", 128, b2), ("LvS", 128, b2), ("Lv", 16, u2), ("accW", 8, f4), ("cntS", 8, f4),
        ("scE", 256, f4), ("keyE", 256, f4), ("ohE", 256, b2), ("scY", 256, f4), ("keyY", 256, f4), ("ohY", 256, b2),
        ("MjS", 256, b2), ("MjW", 256, b2), ("gOj", 256, f4), ("Dj", 256, f4), ("MgS", 272, b2), ("t1", 256, f4), ("An", 256, f4), ("Bm", 256, b2),
        ("Vt", 256, f4), ("NV", 256, b2), ("foeN", 256, b2), ("prevN", 256, b2), ("nn", 256, b2), ("Bt", 256, b2),
        ("ee", 256, b2), ("dg", 256, b2), ("dgs", 256, b2), ("uI", 256, i4), ("suI", 256, i4),
        ("outT", 1024, f4),
        ("Own", 5 * 256, f4), ("foe1", 5 * 256, b2), ("TPs", 5 * 512, b2), ("Lts", 4 * 16, u2), ("u2S", 4 * 256, f4), ("Uc", 4 * 256, b2),
        ("MjO", 4 * 256, f4), ("WinS", 4 * 256, b2), ("prV", 4 * 256, f4), ("prN", 4 * 256, b2),
        ("TPl", 4 * 528, b2), ("Ltl", 4 * 16, u2), ("u2l", 4 * 256, f4), ("Ul", 4 * 256, b2), ("MjOl", 4 * 264, f4),
        ("Winl", 4 * 256, b2), ("prVl", 4 * 256, f4), ("prNl", 4 * 256, b2)):
    SCRATCH[_n] = ("sbuf", [128, _c], _d)
for _i in range(8):
    SCRATCH["ps%d" % _i] = ("psum", [128, 512], f4)
KINDS = ("T", "P", "u", "U", "M", "w", "v", "n")
SEMAPHORES = ["sv", "sa", "sp", "sg", "ls"] + ["d%d" % i for i in range(16)] + ["x%s%d" % (k, t) for k in KINDS for t in range(NR)]
VF = (4, 3)
FILL = (4, 3, 2, 2, 2, 3)
PS = {"KE0": (0, 0, 128), "KY0": (0, 128, 128), "u2P": (0, 256, 256), "KE1": (1, 0, 128), "KY1": (1, 128, 128),
      "D0": (3, 0, 512), "D1": (4, 0, 512), "Urep": (2, 0, 256), "Vrep": (2, 256, 256),
      "loR": (3, 0, 256), "Ft": (3, 0, 256), "cntB": (3, 256, 256), "LvF": (3, 256, 128),
      "HiB": (4, 0, 256), "Fn": (4, 0, 256), "foeQ": (6, 256, 256), "cnt": (2, 0, 1), "LoB": (4, 256, 256), "WinN": (4, 256, 256), "preQ": (7, 256, 256),
      "St": (5, 0, 256), "OjV": (7, 256, 256), "ddP": (7, 0, 256), "nbg": (5, 0, 256), "MjT": (5, 256, 256), "MgT": (5, 256, 256),
      "winR": (6, 0, 256), "foeP": (6, 256, 256), "tauP": (6, 0, 256), "Vg0": (7, 0, 128), "pr0": (7, 256, 128), "foeI": (7, 256, 256), "Vg1": (1, 256, 128), "pr1": (1, 384, 128)}


def rank_program(g, core, T, topo):
    rank = T.rank_of(core)
    if rank is None:
        return
    qs = {"g": g, "v": g.vector, "a": g.scalar, "p": g.tensor, "s": g.sync}
    esem = {"v": "sv", "a": "sa", "p": "sp", "g": "sg"}
    cnt = {}
    known = {q: {} for q in qs}
    snap = {}
    lastw, readers, bank = {}, {}, {}

    def need(q, ev):
        kn = known[q]
        if kn.get(ev[0], 0) >= ev[1]:
            return
        qs[q].wait_ge(T.sem[ev[0]], ev[1])
        for s, v in list(snap.get(ev, {}).items()) + [ev]:
            if kn.get(s, 0) < v:
                kn[s] = v

    def deps(q, R, Wr):
        for k in R:
            w = lastw.get(k)
            if w is not None and not (q == "p" and w[0] == "p"):
                need(q, w[1])
        for k in Wr:
            w = lastw.get(k)
            if w is not None and not (q == "p" and w[0] == "p"):
                need(q, w[1])
            for e, ev in readers.get(k, {}).items():
                if e != q:
                    need(q, ev)
        for k in R + Wr:
            if k in PS:
                for e, ev in bank.get(PS[k][0], {}).items():
                    if e != q:
                        need(q, ev)

    def note(q, ev, R, Wr):
        snap[ev] = dict(known[q])
        for k in R:
            readers.setdefault(k, {})[q] = ev
        for k in Wr:
            lastw[k] = (q, ev)
            readers[k] = {}
        for k in R + Wr:
            if k in PS:
                bank.setdefault(PS[k][0], {})[q] = ev

    def op(q, R, Wr, call):
        R, Wr = R.split(), Wr.split()
        deps(q, R, Wr)
        ins = call(qs[q])
        s = esem[q]
        cnt[s] = cnt.get(s, 0) + 1
        ins.then_inc(T.sem[s], 1)
        note(q, (s, cnt[s]), R, Wr)

    def dma(q, sem, R, Wr, out, in_):
        R, Wr = R.split(), Wr.split()
        deps(q, R, Wr)
        qs[q].dma_start(out=out, in_=in_).then_inc(T.sem[sem], 16)
        cnt[sem] = 16
        snap[(sem, 16)] = dict(known[q])
        for k in Wr:
            lastw[k] = ("dma", (sem, 16))
            readers[k] = {}
        for k in R:
            readers.setdefault(k, {})[sem] = (sem, 16)

    def send(kind, t, dst, R, out, in_):
        deps("g", R.split(), [])
        rid, pid = topo.addr(dst)[:2]
        g.remote_dma(out, in_, T.sem["x%s%d" % (kind, t)], T.sem.ls, pid, rid, topo.mask(core, dst))
        cnt["ls"] = cnt.get("ls", 0) + len(topo.engines(core, dst))

    def expect(kind, t, src, key):
        s = "x%s%d" % (kind, t)
        cnt[s] = len(topo.engines(src, core))
        lastw[key] = ("net", (s, cnt[s]))

    def ps(k, a=0, n=None, step=1):
        b, c, w = PS[k]
        n = w if n is None else n
        return T["ps%d" % b][:, c + a:c + a + n:step] if step > 1 else T["ps%d" % b][:, c + a:c + a + n]

    def sl(k, t, w=256, a=0, n=None):
        n = w if n is None else n
        return T[k][:, t * w + a:t * w + a + n]

    def tt(R, Wr, out, a, b, o, q="v"):
        op(q, R, Wr, lambda e: e.tensor_tensor(out=out, in0=a, in1=b, op=o))

    def ts(R, Wr, out, a, s1, o1, s2=None, o2=None):
        if o2 is None:
            op("v", R, Wr, lambda e: e.tensor_scalar(out=out, in0=a, scalar1=s1, scalar2=None, op0=o1))
        else:
            op("v", R, Wr, lambda e: e.tensor_scalar(out=out, in0=a, scalar1=s1, scalar2=s2, op0=o1, op1=o2))

    def cp(R, Wr, out, a):
        op("v", R, Wr, lambda e: e.tensor_copy(out=out, in_=a))

    def act(R, Wr, out, a, scale=1.0, bias=0.0, func=None, acc=None):
        op("a", R, Wr, lambda e: e.activation(out=out, in_=a, func=F.Copy if func is None else func, bias=bias, scale=scale, accum_out=acc))

    def scan(R, Wr, out, d0, d1, o0, o1):
        op("v", R, Wr, lambda e: e.tensor_tensor_scan(out=out, data0=d0, data1=d1, initial=0.0, op0=o0, op1=o1))

    def mm(R, Wr, out, l, r, start=True, stop=True):
        op("p", R, Wr, lambda e: e.matmul(out, l, r, start, stop))

    def ms(Wr, ap, c):
        op("v", "", Wr, lambda e: e.memset(ap, c))

    def iota(Wr, ap, pattern, base, cm, small=True):
        if small:
            op("g", "", Wr, lambda e: e.iota(ap, pattern, base, cm, allow_small_or_imprecise_dtypes=True))
        else:
            op("g", "", Wr, lambda e: e.iota(ap, pattern, base, cm))

    def peer(k):
        return T.cores[(rank + k) % NR]

    dist = [1 + t % 3 for t in range(NR)]
    for t in range(NR):
        th, vi = peer(-dist[t]), peer(dist[t])
        for kind, src, key in (("T", th, "Ltl"), ("P", th, "TPl"), ("u", th, "u2l"), ("U", th, "Ul"), ("M", th, "MjOl"), ("w", vi, "Winl"), ("v", vi, "prVl"), ("n", vi, "prNl")):
            expect(kind, t, src, "%s%d" % (key, t))

    in8 = T.in8
    dma("s", "d0", "", "in8a", in8[0:8, 0:256], T.tas[:])
    dma("a", "d3", "", "in8b0", in8[0:8, 256:512], T.tau[:])
    dma("s", "d1", "", "ownI", T.ownI[:], T.own[:])
    dma("a", "d4", "", "in8b1", in8[0:8, 512:768], T.prev[:])
    dma("s", "d2", "", "hueA", T.hueS[:, 0:W], T.hue[:])
    dma("a", "d5", "", "in8b2", in8[0:8, 768:1024], T.foe[:])
    dma("s", "d6", "", "hueB", T.hueS[:, W:WX], T.hue[:, 0:WX - W])
    dma("s", "d7", "", "wtI", T.wtI[:, 0:1], T.wt[:])
    dma("s", "d8", "", "nbI", T.nbI[:], T.nb[:])
    C, CI = T.cols, T.colsI
    iota("ci0", CI[:, 0:1], [[0, 1]], 0, 1, False)
    iota("iA", T.iotA[:], [[1, 8], [0, 16]], 0, 0)
    iota("iB", T.iotB[:], [[1, 128]], 0, 0)
    iota("iC", T.iotC[:], [[0, 16], [1, 16]], 0, 0)
    iota("iD", T.iotD[:], [[0, 32], [1, 8]], 0, 0)
    iota("iE", T.iotE[:], [[1, 16], [16, 8]], 0, 0)
    iota("iG", T.iotG[:], [[0, 8], [-1, 16]], 15, 0)
    iota("iH", T.iotH[:], [[16, 16]], 15, 0)
    iota("iJ", T.iotJ[:], [[1, 256]], 1, 0)
    ts("ci0", "ci1", CI[:, 1:2], CI[:, 0:1], 4, A.arith_shift_right)
    ts("ci0", "ci2", CI[:, 2:3], CI[:, 0:1], 15, A.bitwise_and)
    ts("ci0", "ci3", CI[:, 3:4], CI[:, 0:1], 7, A.bitwise_and)
    cp("ci0 ci1 ci2 ci3", "c0", C[:, 0:4], CI[:, 0:4])
    p_, pdiv, pmod, pm8 = C[:, 0:1], C[:, 1:2], C[:, 2:3], C[:, 3:4]
    ts("c0 iA", "E8f", T.E8f[:], T.iotA[:], p_, A.is_equal)
    act("E8f", "E8b", T.E8b[:], T.E8f[:])
    ts("c0 iB", "ident", T.ident[:], T.iotB[:], p_, A.is_equal)
    act("ident", "nident", T.nident[:], T.ident[:], -1.0)
    ms("smask", T.smask[:], 1.0)
    ms("smask", T.smask[:, 0:2048:16], 0.0)
    ts("c0 iC", "dmask", T.dmask[:], T.iotC[:], pmod, A.is_equal)
    ts("c0 iA", "BO", T.BO[:], T.iotA[:], pdiv, A.is_equal)
    cp("in8a", "tasF", T.tasF[0:8, :], in8[0:8, 0:256])
    mm("E8f tasF", "winR", ps("winR"), T.E8f[0:8, :], T.tasF[0:8, :])
    ts("winR", "u2P", ps("u2P"), ps("winR"), 2.0, A.mult, 33.0, A.add)
    act("u2P", "u2S0", sl("u2S", 0), ps("u2P"))
    send("u", 0, peer(dist[0]), "u2S0", sl("u2l", 0), sl("u2S", 0))
    cp("ownI", "Own00 Own01", sl("Own", 0), T.ownI[:])
    for j in range(3):
        cp("in8b%d" % j, "inb%d" % j, T.in8b[0:8, 256 * j:256 * j + 256], in8[0:8, 256 + 256 * j:512 + 256 * j])
    mm("E8b inb0", "tauP", ps("tauP"), T.E8b[0:8, :], T.in8b[0:8, 0:256])
    mm("E8b inb1", "foeP", ps("foeP"), T.E8b[0:8, :], T.in8b[0:8, 256:512])
    mm("E8b inb2", "foeI", ps("foeI"), T.E8b[0:8, :], T.in8b[0:8, 512:768])

    def new_list(t):
        tt("tauP dmask", "dg", T.dg[:], ps("tauP"), T.dmask[:], A.mult)
        scan("dg smask", "dgs", T.dgs[:], T.smask[:, 0:256], T.dg[:], A.mult, A.add)
        cp("dgs", "Lts%d" % t, sl("Lts", t, 16), T.dgs[:, 15:256:16])
        send("T", t, peer(dist[t]), "Lts%d" % t, sl("Ltl", t, 16), sl("Lts", t, 16))

    def home_offsets(t, h):
        x = slice(128 * h, 128 * h + 128)
        tt("Own%d%d u2P" % (t, h), "mI%d" % h, T.mI[:, x], sl("Own", t, 256, 128 * h, 128), ps("u2P", 128 * h, 128), A.mult)
        ts("mI%d" % h, "m2I%d" % h, T.m2I[:, x], T.mI[:, x], 5, A.arith_shift_right, 4095, A.bitwise_and)
        ts("m2I%d" % h, "Hx%d" % h, T.Hx[:, x], T.m2I[:, x], float(77 * t), A.add)
    home_offsets(0, 0)
    home_offsets(0, 1)
    new_list(0)
    act("foeP", "prev0", sl("TPs", 0, 512, 256, 256), ps("foeP"))
    act("foeI", "foe0", sl("foe1", 0), ps("foeI"), 1.0, 1.0)
    ts("c0", "c6", C[:, 6:7], pmod, -16.0, A.mult, 0.5, A.add)
    ts("c0", "c7", C[:, 7:8], pmod, 112.0, A.add)
    ts("c0", "c4", C[:, 4:5], pmod, 0.0, A.is_equal, -1000.0, A.mult)
    ts("c0", "c5", C[:, 5:6], p_, -1.0, A.add)
    tt("c4 c5", "c8", C[:, 8:9], C[:, 4:5], C[:, 5:6], A.add)
    ts("c0", "c9", C[:, 9:10], p_, -256.0, A.add)
    ts("c0", "c10", C[:, 10:11], p_, -128.0, A.add)
    ts("c0", "c13", C[:, 13:14], p_, -1.1, A.mult, 62.0, A.add)
    act("c13", "c11", C[:, 11:12], C[:, 13:14], 1.0, 0.0, F.Exp)
    ts("c11", "c12", C[:, 12:13], C[:, 11:12], -2.0, A.mult)
    act("BO", "nBO8", T.nBO8[:], T.BO[:], -8.0)
    act("ident c12", "dW2", T.dW2[:], T.ident[:], C[:, 12:13])
    act("BO", "BOf", T.BOf[:], T.BO[:])
    act("BO", "nBOf", T.nBOf[:], T.BO[:], -1.0)
    act("BO", "B8p", T.B8p[:], T.BO[:, 0:128:16], 16.0)
    act("BO", "B8n", T.B8n[:], T.BO[:, 0:128:16], -16.0)
    act("iG", "Kc", T.Kc[:], T.iotG[:])
    ts("c0 iE", "Dm", T.Dm[:], T.iotE[:], p_, A.is_equal)
    ts("c8 iE", "Dtmp", T.Dtmp[:], T.iotE[:], C[:, 8:9], A.is_equal)
    tt("Dm Dtmp", "Dm", T.Dm[:], T.Dm[:], T.Dtmp[:], A.subtract)
    ts("Dm", "Dm", T.Dm[:, 120:128], T.Dm[:, 120:128], 2.0, A.mult)
    act("iJ", "lanep1", T.lanep[:, 0:256], T.iotJ[:])

    def mid_constants():
        cp("wtI", "c14", C[:, 14:15], T.wtI[:, 0:1])
        ts("BO c14", "WT", T.WT[:], T.BO[:], C[:, 14:15], A.mult)
        cp("nbI", "nbB", T.nbB[:], T.nbI[:])
        ts("c0 iD", "BO2", T.BO2[:], T.iotD[:], pdiv, A.is_equal)
        for t in range(NR):
            ms("TPz", T.TPl[:, 528 * t + 512:528 * t + 528], 0.0)
            ms("MjOz", T.MjOl[:, 264 * t + 256:264 * t + 264], 0.0)
        ms("lanep", T.lanep[:, 256:272], 0.0)
        ts("iD", "mask8", T.mask8[:], T.iotD[:, 0:128], 0.0, A.is_gt)

    def late_constants():
        ms("onesf", T.onesf[:], 1.0)
        ms("kmask", T.kmask[:], 0.0)
        ms("kmask", T.kmask[:, 0:128:16], -1048576.0)
        cp("iH", "clist", T.clist[:], T.iotH[:])
        ts("c0 iA", "BO2T", T.BO2T[:], T.iotA[:], pm8, A.is_equal)
        ts("iG", "SelU", T.SelU[:], T.iotG[:], 15.0 - min(SY + [15]), A.is_le, 16.0, A.mult)
        tt("SelU BO", "SelU", T.SelU[:], T.SelU[:], T.BO[:], A.mult)
        ms("MgS", T.MgS[:], 0.0)
        ms("negone", T.negone[:], -1.0)

    HU = T.hueS[:, 0:WX]

    for t in range(NR):
        last = t == NR - 1
        thief, victim = peer(-dist[t]), peer(dist[t])
        Ot, Ut, Lt = sl("Own", t), sl("Uc", t), sl("Ltl", t, 16)
        own, uc, ltl, tpl = "Own%d0 Own%d1" % (t, t), "Uc%d" % t, "Ltl%d" % t, "TPl%d" % t
        tau = T.TPl[:, 528 * t:528 * t + 256]
        I, nI = T.ident[:], T.nident[:]
        act("hueA hueB Hx0", "xgA", T.xg[:, 0:2048], HU.indirect(T.Hx[:, 0:128]))
        act("tauP", "tau%d" % t, sl("TPs", t, 512, 0, 256), ps("tauP"))
        if t:
            act("preQ", "prev%d" % t, sl("TPs", t, 512, 256, 256), ps("preQ"))
        send("P", t, victim, "tau%d prev%d" % (t, t), T.TPl[:, 528 * t:528 * t + 512], sl("TPs", t, 512))
        act("hueA hueB Hx1", "xgB", T.xg[:, 2048:16 * XS], HU.indirect(T.Hx[:, 128:XS]))
        cp("hueA hueB Hx1", "xgV", T.xg[:, 16 * XS:4096], HU.indirect(T.Hx[:, XS:256]))
        if t == 0:
            mid_constants()
        scan("xgA smask", "RsA", T.Rs[:, 0:2048], T.smask[:, 0:2048], T.xg[:, 0:2048], A.mult, A.max)
        tt("%s %s u2l%d" % (own, ltl, t), "myI", T.myI[:], Ot.indirect(Lt), sl("u2l", t), A.mult)
        ts("myI", "my2I", T.my2I[:], T.myI[:], 5, A.arith_shift_right, 4095, A.bitwise_and)
        ts("my2I", "Hy", T.Hy[:], T.my2I[:], float(77 * t), A.add)
        act("hueA hueB Hy", "yg0", T.yg[:, 0:1024], HU.indirect(T.Hy[:, 0:64]))
        scan("xgV smask", "RsV", T.Rs[:, 16 * XS:4096], T.smask[:, 0:4096 - 16 * XS], T.xg[:, 16 * XS:4096], A.mult, A.max)
        scan("xgB smask", "RsB", T.Rs[:, 2048:16 * XS], T.smask[:, 0:16 * XS - 2048], T.xg[:, 2048:16 * XS], A.mult, A.max)
        cp("RsV RsA RsB", uc, Ut, T.Rs[:, 15:4096:16])
        send("U", t, victim, uc, sl("Ul", t), Ut)
        mm("ident %s" % uc, "Urep", ps("Urep"), I, Ut)
        for h in range(2):
            mm("ident Kc", "KE%d" % h, ps("KE%d" % h), I, T.Kc[:, 0:128], True, False)
        mm("WT %s" % uc, "St", ps("St"), T.WT[:], Ut)
        act("%s c6" % tpl, "GE", T.GE[:], tau, 1.0, C[:, 6:7], F.Sign)
        mm("ident %s" % tpl, "loR", ps("loR"), I, tau, True, False)
        mm("nBO8 GE", "loR", ps("loR"), T.nBO8[:], T.GE[:], False, True)
        for h in range(2):
            mm("GE Dm", "HiB", ps("HiB", 128 * h, 128), T.GE[:, 128 * h:128 * h + 128], T.Dm[:])
        act("hueA hueB Hy", "yg1", T.yg[:, 1024:2048], HU.indirect(T.Hy[:, 64:128]))
        f1 = sl("foe1", t)
        pv, ta = sl("TPs", t, 512, 256, 256), sl("TPs", t, 512, 0, 256)
        mm("ident tau%d" % t, "ddP", ps("ddP"), I, ta, True, False)
        mm("nident prev%d" % t, "ddP", ps("ddP"), nI, pv, False, True)

        def diff(pair, j, X, Xk, neg, negk, bias, out, outk):
            for i, k in enumerate(pair):
                o = ps("D%d" % (j % 2), 256 * i, 256)
                mm("ident " + Xk, "D%d" % (j % 2), o, I, X[:, k:4096:16], True, False)
                mm("nident " + negk, "D%d" % (j % 2), o, nI, neg, False, True)
            k = pair[0]
            act("D%d" % (j % 2), "%s%d %s%d" % (outk, k, outk, k + 1), out[:, 256 * k:256 * k + 512], ps("D%d" % (j % 2)), 1.0, bias, F.Relu)

        EV, YV = [k for k in range(16) if k not in SE], [k for k in range(16) if k not in SY]
        todo = [("E", k) for k in EV] + [("Y", k) for k in YV]
        wait_sums, left, opened = [], {"E": 16, "Y": 16}, []

        def sums(what, k):
            left[what] -= 1
            K, M = ("KE", T.B8n) if what == "E" else ("KY", T.B8p)
            buf = T.Eb if what == "E" else T.Yb
            for h in range(2):
                mm("%sb%d %s" % (what, k, "B8n" if what == "E" else "B8p"), "%s%d" % (K, h), ps("%s%d" % (K, h), k, 128 - k, 16),
                   buf[:, 256 * k + 128 * h:256 * k + 128 * h + 128], M[:], False, left[what] == 0)

        def ysum(k):
            if opened:
                sums("Y", k)
            else:
                wait_sums.append(k)

        def fill(n):
            for _ in range(n):
                if not todo:
                    return
                what, k = todo.pop(0)
                if what == "E":
                    tt("xgV xgA xgB Urep", "Eb%d" % k, T.Eb[:, 256 * k:256 * k + 256], T.xg[:, k:4096:16], ps("Urep"), A.is_equal)
                    sums("E", k)
                else:
                    tt("yg0 yg1 yg2 Vrep", "Yb%d" % k, T.Yb[:, 256 * k:256 * k + 256], T.yg[:, k:4096:16], ps("Vrep"), A.max)
                    ysum(k)

        dtodo = [("E", SE[i:i + 2]) for i in range(0, len(SE), 2)] + [("Y", SY[i:i + 2]) for i in range(0, len(SY), 2)]
        dn = [0]

        lag = []

        def flush():
            while lag:
                what, k = lag.pop(0)
                if what == "E":
                    sums("E", k)
                else:
                    ysum(k)

        def dfill(n):
            for _ in range(n):
                if not dtodo:
                    return
                what, pair = dtodo.pop(0)
                if what == "E":
                    diff(pair, dn[0], T.xg, "xgV xgA xgB", Ut, uc, 1.0, T.Eb, "Eb")
                else:
                    diff(pair, dn[0], T.yg, "yg0 yg1 yg2", sl("Ul", t), "Ul%d" % t, 0.0, T.Yb, "Yb")
                flush()
                lag.extend((what, k) for k in pair)
                dn[0] += 1

        if t == 0:
            late_constants()
        fill(FILL[0])
        ts("loR c7", "LoT", T.LoT[:], ps("loR"), C[:, 7:8], A.is_equal)
        for h in range(2):
            mm("LoT ident", "LoB", ps("LoB", 128 * h, 128), T.LoT[:, 128 * h:128 * h + 128], I)
        act("HiB", "thrHi", T.thrHi[:], ps("HiB"), 4.5)
        act("LoB c11", "LoW", T.LoW[:], ps("LoB"), C[:, 11:12])
        act("LoB", "LoBig", T.LoBig[:], ps("LoB", 0, 128), float(2.0 ** 93))
        act("LoB c9", "LoWb0", T.LoWb[:, 0:128], ps("LoB", 0, 128), C[:, 9:10])
        act("LoB c10", "LoWb1", T.LoWb[:, 128:256], ps("LoB", 128, 128), C[:, 10:11])
        act("hueA hueB Hy", "yg2", T.yg[:, 2048:4096], HU.indirect(T.Hy[:, 128:256]))
        fill(FILL[5])
        tt("%s %s Ul%d" % (uc, ltl, t), "cmp", T.cmp[:], Ut.indirect(Lt), sl("Ul", t), A.is_gt)
        for h in range(2):
            mm("cmp BO2", "cntB", ps("cntB", 128 * h, 128), T.cmp[:, 128 * h:128 * h + 128], T.BO2[:, 0:128])
        fill(FILL[1])
        tt("cntB thrHi", "OKHi", T.OKHi[:], ps("cntB"), T.thrHi[:], A.is_lt)
        mm("LoW OKHi", "Ft", ps("Ft", 0, 128), T.LoW[:, 0:128], T.OKHi[:, 0:128])
        mm("LoBig OKHi", "Ft", ps("Ft", 128, 128), T.LoBig[:], T.OKHi[:, 0:128], True, False)
        mm("LoW OKHi", "Ft", ps("Ft", 128, 128), T.LoW[:, 128:256], T.OKHi[:, 128:256], False, True)
        fill(FILL[2])
        tt("Ft BO2", "Fm", T.Fm[:], ps("Ft"), T.BO2[:], A.mult)
        for h in range(2):
            mm("dW2 OKHi", "Fn", ps("Fn", 128 * h, 128), T.dW2[:], T.OKHi[:, 128 * h:128 * h + 128], True, False)
            mm("LoT Fm", "Fn", ps("Fn", 128 * h, 128), T.LoT[:, 128 * h:128 * h + 128], T.Fm[:, 128 * h:128 * h + 128], False, True)
        fill(FILL[3])
        ts("Fn", "Win", T.Win[:], ps("Fn"), 0.0, A.is_lt)
        for h in range(2):
            mm("LoWb%d Win" % h, "LvF", ps("LvF"), T.LoWb[:, 128 * h:128 * h + 128], T.Win[:, 128 * h:128 * h + 128], h == 0, h == 1)
        for h in range(2):
            mm("Win ident", "WinN", ps("WinN", 128 * h, 128), T.Win[:, 128 * h:128 * h + 128], T.ident[:])
        act("WinN", "WinS%d accW" % t, sl("WinS", t), ps("WinN"), acc=T.accW[:, 0:1])
        send("w", t, thief, "WinS%d" % t, sl("Winl", t), sl("WinS", t))
        fill(FILL[4])
        tt("LvF BO2", "LvM", T.LvM[:], ps("LvF"), T.BO2[:, 0:128], A.mult)
        scan("LvM mask8", "LvS", T.LvS[:], T.mask8[:], T.LvM[:], A.mult, A.add)
        ts("LvS", "Lv", T.Lv[:], T.LvS[:, 7:128:8], 256.0, A.add)
        while [x for x in todo if x[0] == "E"] or [x for x in dtodo if x[0] == "E"]:
            if dtodo and dtodo[0][0] == "E":
                dfill(1)
            fill(2)
        if SE:
            flush()
        mm("ident Ul%d" % t, "Vrep", ps("Vrep"), I, sl("Ul", t))

        def best(e):
            for h in range(2):
                x, y = slice(128 * h, 128 * h + 128), slice(128 - 128 * h, 256 - 128 * h)
                act("K%s%d" % (e, h), "key%s%d" % (e, h), T["key" + e][:, x], ps("K%s%d" % (e, h)))
                scan("K%s%d kmask" % (e, 1 - h), "sc%s%d" % (e, 1 - h), T["sc" + e][:, y], T.kmask[:, 0:128], ps("K%s%d" % (e, 1 - h)), A.add, A.max)
            tt("sc%s0 sc%s1 key%s0 key%s1 clist" % (e, e, e, e), "oh" + e, T["oh" + e][:], T["sc" + e][:].indirect(T.clist[:]), T["key" + e][:], A.is_equal)
        best("E")
        act("lanep lanep1 Lv", "foeN", T.foeN[:], T.lanep[:].indirect(T.Lv[:]))
        act("foeN", "nn", T.nn[:], T.foeN[:], -1.0, 1.0, F.Relu)
        dfill(1)
        for h in range(2):
            mm("ohE ident", "MjT", ps("MjT", 128 * h, 128), T.ohE[:, 128 * h:128 * h + 128], T.ident[:])
        mm("onesf accW", "cnt", ps("cnt"), T.onesf[:], T.accW[:, 0:1])
        if t:
            act("foeQ", "foe%d" % t, f1, ps("foeQ"))
        dfill(1)
        act("ddP", "dd", T.dd[:], ps("ddP"))
        act("%s TPz Lv" % tpl, "prevN", T.prevN[:], T.TPl[:, 528 * t + 256:528 * t + 528].indirect(T.Lv[:]))
        mm("ident foe%d" % t, "foeP", ps("foeP"), I, f1)
        for h in range(2):
            mm("ident Kc", "KY%d" % h, ps("KY%d" % h), I, T.Kc[:, 0:128], True, False)
            mm("Ul%d SelU" % t, "KY%d" % h, ps("KY%d" % h), T.Ul[:, 256 * t + 128 * h:256 * t + 128 * h + 128], T.SelU[:], False, False)
        opened.append(1)
        dfill(1)
        for k in wait_sums:
            sums("Y", k)
        tt("MjT %s" % own, "MjO%d" % t, sl("MjO", t), ps("MjT"), Ot, A.mult)
        send("M", t, victim, "MjO%d" % t, T.MjOl[:, 264 * t:264 * t + 256], sl("MjO", t))
        act("MjT", "MjS", T.MjS[:], ps("MjT"))
        fill(VF[0])
        mm("BO2T Winl%d" % t, "winR", ps("winR"), T.BO2T[:], sl("Winl", t))
        act("%s %s" % (own, ltl), "Vt", T.Vt[:], Ot.indirect(Lt))
        dfill(1)
        act("nbB %s" % ltl, "NV", T.NV[:], T.nbB[:].indirect(Lt))
        fill(VF[1])
        tt("foeP nn", "nf", T.nf[:], ps("foeP"), T.nn[:], A.mult)
        tt("winR nn", "Bt", T.Bt[:], ps("winR"), T.nn[:], A.mult)
        tt("winR dd", "wd", T.wd[:], ps("winR"), T.dd[:], A.mult)
        tt("winR MjS", "MjW", T.MjW[:], ps("winR"), T.MjS[:], A.mult)
        while todo or dtodo:
            dfill(1)
            fill(2)
        flush()
        best("Y")
        act("MjOl%d MjOz Lv" % t, "gOj", T.gOj[:], T.MjOl[:, 264 * t:264 * t + 264].indirect(T.Lv[:]))
        for h in range(2):
            mm("ohY ident", "MgT", ps("MgT", 128 * h, 128), T.ohY[:, 128 * h:128 * h + 128], T.ident[:])
        mm("BOf gOj", "OjV", ps("OjV"), T.BOf[:], T.gOj[:])
        tt("MgT Vt", "prV%d" % t, sl("prV", t), ps("MgT"), T.Vt[:], A.mult)
        send("v", t, thief, "prV%d" % t, sl("prVl", t), sl("prV", t))
        tt("MgT NV", "prN%d" % t, sl("prN", t), ps("MgT"), T.NV[:], A.mult)
        send("n", t, thief, "prN%d" % t, sl("prNl", t), sl("prN", t))
        act("MgT", "MgS", T.MgS[:, 0:256], ps("MgT"))
        tt("OjV %s" % own, "Dj", T.Dj[:], ps("OjV"), Ot, A.subtract)
        tt("MgS Lv Dj", "t1", T.t1[:], T.MgS[:].indirect(T.Lv[:]), T.Dj[:], A.mult)
        tt("MgS Lv MjW", "Bm", T.Bm[:], T.MgS[:].indirect(T.Lv[:]), T.MjW[:], A.is_lt)
        tt("t1 %s" % own, "An", T.An[:], T.t1[:], Ot, A.add)
        cp("cnt", "cntS", T.cntS[:, 0:1], ps("cnt"))
        ts("St cntS", "suI", T.suI[:], ps("St"), T.cntS[:, 0:1], A.add)
        ts("suI", "uI", T.uI[:], T.suI[:], 1023, A.bitwise_and)
        if not last:
            ts("uI", "u2P", ps("u2P"), T.uI[:], 2.0, A.mult, 33.0, A.add)
            act("u2P", "u2S%d" % (t + 1), sl("u2S", t + 1), ps("u2P"))
            send("u", t + 1, peer(dist[t + 1]), "u2S%d" % (t + 1), sl("u2l", t + 1), sl("u2S", t + 1))
        else:
            cp("uI", "outU", T.outT[:, 768:1024], T.uI[:])
            dma("s", "d9", "outU", "yu", T.yu[:], T.outT[0:128:16, 768:1024])

        def prev_foe():
            mm("ident prev%d" % t, "preQ", ps("preQ"), I, pv, True, False)
            mm("ident wd", "preQ", ps("preQ"), I, T.wd[:], False, True)
            mm("ident nf", "foeQ", ps("foeQ"), I, T.nf[:], True, False)
            mm("ident foeN", "foeQ", ps("foeQ"), I, T.foeN[:], False, True)
        if last:
            prev_foe()
            act("foeQ", "outF", T.outT[:, 512:768], ps("foeQ"), 1.0, -1.0)
            act("preQ", "outP", T.outT[:, 256:512], ps("preQ"))
            dma("s", "d10", "outF", "yf", T.yf[:], T.outT[0:128:16, 512:768])
            dma("s", "d11", "outP", "yp", T.yp[:], T.outT[0:128:16, 256:512])
        for h in range(2):
            mm("nBOf MjO%d" % t, "Vg%d" % h, ps("Vg%d" % h), T.nBOf[:], sl("MjO", t, 256, 128 * h, 128), True, False)
        mm("ident prevN", "tauP", ps("tauP"), I, T.prevN[:], True, False)
        mm("ident nf", "tauP", ps("tauP"), I, T.nf[:], False, False)
        mm("nident nn", "tauP", ps("tauP"), nI, T.nn[:], False, False)
        mm("nident foe%d" % t, "nbg", ps("nbg"), nI, f1, True, False)
        mm("nident negone", "nbg", ps("nbg"), nI, T.negone[:], False, False)
        for h in range(2):
            mm("BOf prVl%d" % t, "Vg%d" % h, ps("Vg%d" % h), T.BOf[:], sl("prVl", t, 256, 128 * h, 128), False, True)
        mm("BO prNl%d" % t, "nbg", ps("nbg"), T.BO[:], sl("prNl", t), False, True)
        for h in range(2):
            x = slice(128 * h, 128 * h + 128)
            tt("Vg%d Bm" % h, "pr%d" % h, ps("pr%d" % h), ps("Vg%d" % h), T.Bm[:, x], A.mult)
            tt("pr%d An" % h, "Own%d%d" % (t + 1, h), sl("Own", t + 1, 256, 128 * h, 128), ps("pr%d" % h), T.An[:, x], A.add)
            if not last:
                home_offsets(t + 1, h)
        if last:
            dma("s", "d12", "Own40 Own41", "yo", T.yo[:], sl("Own", 4))
        tt("nbg Bt", "ee", T.ee[:], ps("nbg"), T.Bt[:], A.mult)
        mm("ident ee", "tauP", ps("tauP"), I, T.ee[:], False, True)
        if not last:
            new_list(t + 1)
            prev_foe()
        else:
            act("tauP", "outTau", T.outT[:, 0:256], ps("tauP"))
            dma("s", "d13", "outTau", "yt", T.yt[:], T.outT[0:128:16, 0:256])
    for s in sorted(cnt):
        need("s", (s, cnt[s]))
